import numpy as np, ml_dtypes
CORES = [40,41,42,43,44,45,46,47]
N = 8
BF = ml_dtypes.bfloat16
Y, X, O, S, Q, R = 32, 128, 512, 2, 256, 5
PL = Y * X
def plain(rng):
    u = 0.5 - 0.5 * np.cos(np.pi * rng.random((N, 8, 16, O)))
    v = np.where((np.arange(8) % 2 == 0)[None, :, None, None], 0.25 + 3.75 * u, (0.5 + 1.5 * u) * np.exp2(rng.integers(-1, 2, (N, 8, 16, 1))))
    return v, rng.integers(0, 16, (N, 8, 16, O)), rng.integers(-7, 8, (N, 3, 128, 128))
def pack(v, z, a):
    a = a.astype(np.float32).astype(BF)
    return {"v0": np.ascontiguousarray(np.clip(v, 0.25, 4.0).reshape(N, 128, O)).astype(np.float32).astype(BF), "z0": np.ascontiguousarray(z.reshape(N, 128, O)).astype(np.float32).astype(BF),
            "ay": np.ascontiguousarray(a[:, 0]), "ax": np.ascontiguousarray(a[:, 1]), "bm": np.ascontiguousarray(a[:, 2])}
def slip():
    s0 = np.arange(208, 256) * 2.0 ** -6; e = np.repeat(s0[None, :], S, axis=0); b = e.copy()
    for t in range(R):
        p = t % S; o = (t - 1) % S
        e[p] = 0.5 * e[p] + 0.25 * np.exp(-np.minimum(0.125 * np.abs(e[p] - e[o]), 0.25)) * e[o]
        c = b.astype(np.float32).astype(BF).astype(np.float64)
        b[p] = 0.5 * b[p] + 0.25 * np.exp(-np.minimum(0.125 * np.abs(c[p] - c[o]), 0.25)) * b[o]
    return s0, np.max(np.abs(e - b), axis=0)
def setup_inputs(rng):
    return pack(*plain(rng))
def setup_inputs_spread(rng):
    v, z, a = plain(rng)
    v = (0.5 + 1.5 * rng.random((N, 8, 16, O))) * np.exp2(rng.integers(-1, 2, (N, 8, 1, O)))
    z = np.minimum((16 * rng.random((N, 8, 16, O)) ** rng.choice(np.array([0.25, 1.0, 4.0]), (N, 8, 16, 1))).astype(np.int64), 15)
    cap = rng.integers(1, 8, (N, 3, 1, 128)); share = rng.choice(np.array([0.2, 0.6, 1.0]), (N, 3, 1, 128))
    a = np.clip(a, -cap, cap) * (rng.random(a.shape) < share)
    return pack(v, z, a)
def setup_inputs_ends(rng):
    base = rng.random((1, 8, 16, 1)) < 0.5
    flip = (rng.random((N, 8, 16, O)) < 1 / 8) ^ (rng.random((N, 8, 1, O)) < 1 / 16)
    flip[:, :, :, 0] = False; flip[:, :, :, O - 1] = True
    v = np.where(base ^ flip, 4.0, 0.25)
    full = np.array([0, O // 2 + 1, O - 2, O - 1]); less = np.array([2, 3, 4, 5, O - 5, O - 4])
    dens = rng.choice(np.array([0, 1 / 32, 1 / 8, 1.0]), (N, 1, 1, O), p=np.array([0.05, 0.55, 0.36, 0.04])); dens[..., full] = 1.0; dens[..., np.array([1, O - 3])] = 0.0; dens[..., less] = 1.0
    z = 15 * (rng.random((N, 8, 16, O)) < dens)
    m = np.where((dens == 1.0) & (rng.random(dens.shape) < 0.5), rng.integers(1, 41, dens.shape), 0); m[..., full] = 0; m[..., less] = 1
    z = np.where(np.argsort(rng.random((N, 128, O)), axis=1).reshape(N, 8, 16, O) < m, 0, z)
    a = rng.choice(np.array([-7, 7]), (N, 3, 128, 128))
    a[:, :2, :, 5::16] = np.where(np.argsort(rng.random((N, 2, 128, 8)), axis=2) < 64, 7, -7)
    a[:, 0, :, 127] = 7; a[:, 1, :, 127] = -7; a[:, 0, :, 0] = -7; a[:, 1, :, 0] = 7; a[:, :2, :, 50] = 7; a[:, :2, :, 81] = -7
    a[:, 2, :, 127] = 7; a[:, 2, :, 126] = -7; a[:, 2, :, 1] = 7; a[:, 2, :, 64] = -7
    return pack(v, z, a)
def setup_inputs_near(rng):
    v, z, a = plain(rng)
    cand = np.arange(60, 340); w = np.exp(-cand * 2.0 ** -13); off = np.abs(w - w.astype(np.float32).astype(BF).astype(np.float64))
    n = rng.choice(cand[np.argsort(-off)[:24]], 8)[:, None]
    mag = rng.integers(80, 112, (8, 16)); dif = (n // 16 + (np.arange(16)[None, :] < n % 16)) * rng.choice(np.array([-1, 1]), (8, 16))
    half = ((np.arange(8) // 2 + int(rng.integers(0, 2))) % 2 == 1)[:, None]
    far = half & (np.argsort(rng.random((8, 16)), axis=1) < 14); i = rng.integers(0, 25, (8, 16)); j = rng.integers(0, 8, (8, 16))
    one = np.where(far, (388 + 2 * i + 4 * j) * 2.0 ** -7, mag * 2.0 ** -6)
    two = np.where(far, (129 + 2 * i) * 2.0 ** -7, np.where(half, mag, mag + dif) * 2.0 ** -6)
    share = np.where(np.arange(8) % 2 == 0, 0.5, 0.1)[None, :, None, None]
    kind = rng.random((N, 8, 1, O)) < share
    v = np.where(kind, two[None, :, :, None], one[None, :, :, None])
    for g in np.flatnonzero(half): a[:, 1, :, 16 * g:16 * g + 16] = 0
    return pack(v, z, a)
def setup_inputs_corners(rng):
    v, z, a = plain(rng); sh = int(rng.integers(0, 8)); i16 = np.arange(16)
    for g in range(8):
        k = (g + sh) % 8; lo = 16 * g; hi = lo + 16; at = 16 * ((g + 3) % 8)
        if k == 0: v[:, g] = 0.25 + 0.0625 * v[:1, g, :, :1]
        elif k == 1: v[:, g] = 0.25
        elif k == 2: v[:, g] = np.where((rng.random((N, 1, O)) < 0.5) ^ (rng.random((1, 16, 1)) < 0.5), 1.0, 0.25)
        elif k == 3: v[:, g] = 0.25 + 0.1875 * v[:, g]; v[:, g, 1:] = 0.25
        else: v[:, g] = 1.0 + rng.random((N, 16, O))
        for q in range(N):
            c = (g + q + sh) % 8
            if c == 0: a[q, :2, :, lo:hi] = 0
            elif c == 1: a[q, :2, :, lo:hi] = a[q, :2, :, lo:lo + 1].copy()
            elif c == 2 or c == 3:
                a[q, :2, :, lo:hi] = 0
                for j in range(2): a[q, j, rng.integers(0, 128, 16), lo + i16] = -1 if c == 2 else 1
            elif c == 4: a[q, 0, :, lo:hi] = 0
            elif c == 5: a[q, 1, :, lo:hi] = 0
            elif c == 6:
                w = (1 + (q // 2) % (N - 1)) * (O // X)
                a[q, 0, :, lo:hi] = 0; a[q, 0, at:at + 16, lo:hi] = (w // 16 + (i16 < w % 16))[:, None]
            else:
                a[q, :2, :, lo:hi] = 0; a[q, 1, at:at + 12, lo:hi] = -7; a[q, 0, at + 12:at + 16, lo:hi] = -7
            e = (c + 3) % 8
            if e == 0: z[q, g] = 0
            elif e == 1: z[q, g] = 15
            elif e == 2: z[q, g] = rng.integers(7, 9, (16, O))
            elif e == 3: z[q, g] = rng.integers(0, 2, (16, O))
            elif e == 4:
                z[q, g] = 8
                if q % 2 == 1: z[q, g, :, S * int(rng.integers(0, Q)):][:, :S] = 0
            elif e == 5:
                nx = 8 * (np.arange(O) % X + q % 2) // 7; ny = 8 * (np.arange(O) // X + q % 2) // 7
                z[q, g, :12] = nx[None, :] // 12 + (np.arange(12)[:, None] < nx[None, :] % 12)
                z[q, g, 12:] = ny[None, :] // 4 + (np.arange(4)[:, None] < ny[None, :] % 4)
            b = (c + 6) % 8
            if b == 0: a[q, 2, :, lo:hi] = 0
            elif b == 1 or b == 2:
                a[q, 2, :, lo:hi] = 0; a[q, 2, rng.integers(0, 128, 16), lo + i16] = 1 if b == 1 else -1
            elif b == 3: a[q, 2, :, lo:hi] = 7
    return pack(v, z, a)
def setup_inputs_calm(rng):
    v, z, a = plain(rng); sh = int(rng.integers(0, 8)); i16 = np.arange(16); a[:, 2] = 0
    lev = np.ones(S)
    for t in range(R): lev[t % S] = 0.5 * lev[t % S] + 0.25 * np.mean(lev)
    v = 0.285 / np.sqrt(np.mean(lev * lev)) * (0.8 + 0.4 * rng.random((N, 8, 16, O)))
    s0, far = slip(); alike = float(rng.choice(s0[np.argsort(-far)[:6]]))
    owner = int(rng.integers(0, N)); pick = (np.arange(O) // S) % 16 == int(rng.integers(0, 16)); at = 16 * ((7 - sh) % 8); st = O // X
    for g in range(8):
        h = (g + sh) % 8; lo = 16 * g; hi = lo + 16
        for q in range(N): a[q, 2, lo + (i16 if h == 7 else rng.integers(0, 16, 16)), lo + i16] = 1 if h < 4 else 4
        u = rng.random((N, 16, O))
        if h < 4: z[:, g] = rng.integers(4 * h, 4 * h + 4, (N, 16, O))
        elif h < 6: z[:, g] = np.where(u < 0.0625, 15, np.where(u < 0.75, 14, 13))
        elif h == 6: z[:, g] = np.where(u < 0.01, 3, np.where(u < 0.03, 2, np.where(u < 0.08, 1, 0)))
        else: z[:, g] = 8 * ((i16[:, None] < 10) | pick[None, :])
        if h in (0, 1, 2, 7): a[:, :2, :, lo:hi] = 0
        for q in range(N):
            if h == 0:
                v[q, g] = 4.0 if q % 2 == 0 else 0.25
                if q % 2 == 1: a[q, 0, at + 10:at + 16, lo:hi] = (st // 6 + (np.arange(6) < st % 6))[:, None]
            elif h == 1:
                w = ((owner - q) % N) * st
                if 2 * w > Y: w = w - Y
                a[q, 0, at:at + 10, lo:hi] = (w // 10 + (np.arange(10) < w % 10))[:, None]
                a[q, 1, at:at + 10, lo:hi] = np.arange(10)[:, None] < (i16 % S)[None, :]
            elif h == 2 and q % 2 == 0:
                v[q, g] = alike; a[q, 1, at, lo:hi] = -1
    return pack(v, z, a)
def check_ranges(d):
    bad = []
    for k, lo, hi, w in (("v0", 0.25, 4, False), ("z0", 0, 15, True), ("ay", -7, 7, True), ("ax", -7, 7, True), ("bm", -7, 7, True)):
        a = np.asarray(d[k]).astype(np.float32)
        if not np.all((a >= lo) & (a <= hi)): bad.append("range of " + k)
        elif w and np.any(a != np.floor(a)): bad.append("whole numbers in " + k)
    return bad
def reference(v0, z0, ay, ax, bm):
    V = np.ascontiguousarray(v0.astype(np.float64).transpose(1, 0, 2)).reshape(8, 16, PL)
    z = np.ascontiguousarray(z0.astype(np.float32).astype(np.int64).transpose(1, 0, 2)).reshape(8, 16, PL)
    cy, cx, cb = [a.astype(np.float32).astype(np.int64).transpose(0, 2, 1) for a in (ay, ax, bm)]
    for t in range(R):
        nv = V.copy(); nz = z.copy()
        for r in range(N):
            own = r * O + S * np.arange(Q) + t % S
            zq = z.reshape(128, PL)[:, own]; vq = V[:, :, own]
            dy = np.matmul(cy[r], zq) >> 3; dx = np.matmul(cx[r], zq) >> 3
            pl = X * ((own // X + dy) & (Y - 1)) + ((own % X + dx) & (X - 1))
            ix = pl.reshape(8, 1, 16 * Q)
            m = np.max(np.take_along_axis(z, ix, 2).reshape(8, 16, 16, Q), axis=2).reshape(128, Q)
            nz[:, :, own] = ((np.matmul(cb[r], m) >> 2) & 15).reshape(8, 16, Q)
            vs = np.take_along_axis(V, ix, 2).reshape(8, 16, 16, Q)
            d = np.minimum(0.0078125 * np.sum(np.abs(vq[:, :, None, :] - vs), axis=1), 0.25)
            nv[:, :, own] = 0.5 * vq + 0.015625 * np.sum(np.exp(-d)[:, None] * vs, axis=2)
        V, z = nv, nz
    return {"yv": np.ascontiguousarray(V.reshape(128, N, O).transpose(1, 0, 2)).astype(np.float32), "yz": np.ascontiguousarray(z.reshape(128, N, O).transpose(1, 0, 2)).astype(np.float32)}

def check_inputs(d):
    bad = list(check_ranges(d))
    if not bad:
        for name, y in reference(**d).items():
            for q in range(N):
                v = np.abs(np.asarray(y[q], np.float64)); s = np.sqrt(np.mean(v * v))
                if v.max() > 5 * s or s < 2.0 ** -3: bad.append('%s of rank %d is uneven or too small' % (name, q))
    return bad

@@ -1,0 +1,443 @@
+import math
+from concourse.bass import DstId, RemoteDMATransfer
+from concourse.mybir import AluOpType as ALU, ActivationFunctionType as ACT
+
+R = 5
+NR = 8
+
+SCRATCH = {
+    "vnat": ("sbuf", [128, 4096], "bfloat16"),
+    "znat": ("sbuf", [128, 4096], "bfloat16"),
+    "vw": ("sbuf", [128, 5 * 2048], "float32"),
+    "zw": ("sbuf", [128, 5 * 2048], "bfloat16"),
+    "dif": ("sbuf", [128, 4096], "float32"),
+    "ab": ("sbuf", [128, 4096], "float32"),
+    "zg": ("sbuf", [128, 4096], "bfloat16"),
+    "zs": ("sbuf", [128, 4096], "bfloat16"),
+    "msk": ("sbuf", [128, 2048], "bfloat16"),
+    "vrep": ("sbuf", [128, 2048], "float32"),
+    "off": ("sbuf", [128, 5 * 256], "uint16"),
+    "prm": ("sbuf", [128, 16], "uint16"),
+    "permf": ("sbuf", [128, 16], "float32"),
+    "eT": ("sbuf", [128, 512], "float32"),
+    "eI": ("sbuf", [128, 512], "int32"),
+    "yI": ("sbuf", [128, 256], "int32"),
+    "uI": ("sbuf", [128, 256], "int32"),
+    "sI": ("sbuf", [128, 256], "int32"),
+    "tI": ("sbuf", [128, 256], "int32"),
+    "bI": ("sbuf", [128, 256], "int32"),
+    "cI": ("sbuf", [128, 256], "int32"),
+    "pI": ("sbuf", [128, 8], "int32"),
+    "pF": ("sbuf", [128, 8], "float32"),
+    "row": ("sbuf", [128, 128], "float32"),
+    "row2": ("sbuf", [128, 128], "float32"),
+    "idn": ("sbuf", [128, 128], "float32"),
+    "hd": ("sbuf", [128, 8], "float32"),
+    "big": ("sbuf", [128, 2048], "bfloat16"),
+    "sal": ("sbuf", [128, 128], "bfloat16"),
+    "c32": ("sbuf", [128, 128], "bfloat16"),
+    "posL": ("sbuf", [128, 128], "bfloat16"),
+    "posR": ("sbuf", [128, 512], "bfloat16"),
+    "axy": ("sbuf", [128, 256], "bfloat16"),
+    "bms": ("sbuf", [128, 128], "bfloat16"),
+    "lhs": ("sbuf", [128, 256], "bfloat16"),
+    "rT": ("sbuf", [128, 256], "float32"),
+    "whi": ("sbuf", [128, 256], "bfloat16"),
+    "wlo": ("sbuf", [128, 256], "bfloat16"),
+    "tq": ("sbuf", [128, 256], "float32"),
+    "ovb": ("sbuf", [128, 512], "float32"),
+    "ozb": ("sbuf", [128, 512], "float32"),
+    "W0": ("psum", [128, 512], "float32"),
+    "W1": ("psum", [128, 512], "float32"),
+    "W2": ("psum", [128, 512], "float32"),
+    "W3": ("psum", [128, 512], "float32"),
+    "ST": ("psum", [128, 512], "float32"),
+    "RB": ("psum", [128, 512], "float32"),
+    "FB": ("psum", [128, 512], "float32"),
+    "EB": ("psum", [128, 512], "float32"),
+}
+SEMAPHORES = (["pe", "dve", "act", "pool", "sent", "ldv", "ldz", "ldy", "ldx", "ldb", "st0", "st1", "st2", "vn", "zn"]
+              + ["av%d" % i for i in range(4)] + ["az%d" % i for i in range(4)])
+
+
+def rank_program(g, core, T, topo):
+    r = T.rank_of(core)
+    if r is None:
+        return
+    Q = {"pe": g.tensor, "dve": g.vector, "act": g.scalar, "pool": g, "sp": g.sync}
+    V, A, P = g.vector, g.scalar, g.tensor
+    cnt = {"pe": 0, "dve": 0, "act": 0, "pool": 0, "sent": 0}
+    clock = {q: {} for q in Q}
+    writer, readers, touch = {}, {}, {}
+
+    def sync(q, reads, writes, banks):
+        need = []
+        for x in reads:
+            need += writer.get(x, [])
+        for x in writes:
+            need += writer.get(x, []) + readers.get(x, [])
+        for b in banks:
+            need += [tok for e, tok in touch.get(b, {}).items() if e != q]
+        best = {}
+        for tok in need:
+            if q == "pe" and tok[0] == "pe":
+                continue
+            if tok[0] not in best or best[tok[0]][1] < tok[1]:
+                best[tok[0]] = tok
+        ck = clock[q]
+        for tok in sorted(best.values(), key=lambda k: -len(k[2])):
+            if ck.get(tok[0], 0) >= tok[1]:
+                continue
+            Q[q].wait_ge(T.sem[tok[0]], tok[1])
+            for s, v in tok[2].items():
+                if ck.get(s, 0) < v:
+                    ck[s] = v
+
+    def note(q, tok, reads, writes, banks):
+        for x in reads:
+            readers.setdefault(x, []).append(tok)
+        for x in writes:
+            writer[x] = [tok]
+            readers[x] = []
+        for b in banks:
+            touch.setdefault(b, {})[q] = tok
+
+    def op(q, emit, reads=(), writes=(), banks=()):
+        if q == "pool":
+            writes = list(writes) + ["poolq"]
+        sync(q, reads, writes, banks)
+        emit().then_inc(T.sem[q], 1)
+        cnt[q] += 1
+        ck = dict(clock[q])
+        ck[q] = cnt[q]
+        note(q, (q, cnt[q], ck), reads, writes, banks)
+
+    def dma(q, sem, out, in_, reads=(), writes=()):
+        sync(q, reads, writes, ())
+        Q[q].dma_start(out, in_).then_inc(T.sem[sem], 16)
+        ck = dict(clock[q])
+        ck[sem] = 16
+        note(q, (sem, 16, ck), reads, writes, ())
+
+    peers = [T.cores[(r + j) % NR] for j in range(1, NR)]
+    emask = topo.mask(core, peers[0])
+    for c in peers[1:]:
+        emask &= topo.mask(core, c)
+    neng = bin(emask).count("1")
+    ids = [DstId(rid=topo.addr(c)[0], pnc=topo.addr(c)[1]) for c in peers]
+
+    def send(ap, sem, reads):
+        sync("pool", reads, (), ())
+        g.remote_dma_fused([RemoteDMATransfer(dst_ids=ids, dma_engine_mask=emask, remote_sem=T.sem[sem], src=ap,
+                                              dsts=[ap] * len(ids))], local_sem=T.sem.sent)
+        cnt["sent"] += neng
+
+    def arrivals(name, sem, n):
+        writer[name] = [(sem, n * neng * (NR - 1), {sem: n * neng * (NR - 1)})]
+
+    arrivals("vnat_r", "vn", 1)
+    arrivals("znat_r", "zn", 1)
+    for t in range(R - 1):
+        arrivals("vs%d_r" % (t + 1), "av%d" % t, 2)
+        arrivals("zs%d_r" % (t + 1), "az%d" % t, 1)
+
+    def vec(emit, reads=(), writes=(), banks=()):
+        op("dve", emit, reads, writes, banks)
+
+    def act(emit, reads=(), writes=(), banks=()):
+        op("act", emit, reads, writes, banks)
+
+    def pe(mms, reads=(), banks=()):
+        def emit():
+            last = None
+            for m in mms:
+                last = P.matmul(*m)
+            return last
+        op("pe", emit, reads, (), banks)
+
+    def ps(name):
+        return "ps_" + name
+
+    own = 512 * r
+    dma("sp", "ldv", T.vnat[:, own:own + 512], T.v0[:], (), ["vnat_o"])
+    dma("act", "ldz", T.znat[:, own:own + 512], T.z0[:], (), ["znat_o"])
+    dma("sp", "ldy", T.axy[:, 0:128], T.ay[:], (), ["ay"])
+    dma("act", "ldx", T.axy[:, 128:256], T.ax[:], (), ["ax"])
+    dma("sp", "ldb", T.bms[:], T.bm[:], (), ["bm"])
+
+    vec(lambda: V.memset(T.posR[:], 0.0), (), ["posR"])
+    vec(lambda: V.memset(T.posL[:], 0.0), (), ["posL"])
+    op("pool", lambda: g.iota(T.pI[:, 0:1], [[0, 1]], 0, 1), (), ["p0"])
+    op("pool", lambda: g.iota(T.row[:], [[1, 128]], 0, 0, allow_small_or_imprecise_dtypes=True), (), ["row"])
+    op("pool", lambda: g.iota(T.permf[:], [[128, 2], [2, 8]], 0, 0, allow_small_or_imprecise_dtypes=True), (), ["permf"])
+    op("pool", lambda: g.iota(T.posR[32:33, :], [[256, 16], [0, 2], [16, 16]], 0, 0, allow_small_or_imprecise_dtypes=True),
+       ["posR"], ["posRx"])
+    vec(lambda: V.memset(T.msk[:], 1.0), (), ["msk"])
+    for q4 in range(4):
+        vec(lambda q4=q4: V.memset(T.posR[0:1, 128 * q4:128 * q4 + 128], float(64 * (4 * r + q4))), ["posR"], ["posRy%d" % q4])
+    vec(lambda: V.memset(T.posR[64:65, :], 1.0), ["posR"], ["posR1"])
+    vec(lambda: V.memset(T.posL[0:1, 0:128:2], 1.0), ["posL"], ["posL0"])
+    vec(lambda: V.memset(T.posL[32:33, 1:128:2], 1.0), ["posL"], ["posL1"])
+    vec(lambda: V.memset(T.posL[64:65, 1:128:2], 8.0), ["posL"], ["posL2"])
+    vec(lambda: V.memset(T.msk[:, 0:2048:16], 0.0), (), ["msk"])
+    POS = ["posRx", "posR1", "posL0", "posL1", "posL2"] + ["posRy%d" % i for i in range(4)]
+    vec(lambda: V.tensor_scalar(T.pI[:, 1:2], T.pI[:, 0:1], 7, None, ALU.bitwise_and), ["p0"], ["p1"])
+    vec(lambda: V.tensor_scalar(T.pI[:, 2:3], T.pI[:, 0:1], 4, None, ALU.arith_shift_right), ["p0"], ["p2"])
+    vec(lambda: V.tensor_scalar(T.pI[:, 3:4], T.pI[:, 0:1], 3, 1, ALU.arith_shift_right, ALU.bitwise_and), ["p0"], ["p3"])
+    vec(lambda: V.tensor_copy(T.pF[:, 0:4], T.pI[:, 0:4]), ["p0", "p1", "p2", "p3"], ["pF"])
+    act(lambda: A.activation(T.c32[:], T.row[:], ACT.Exp, bias=-math.log(32.0), scale=0.0), ["row"], ["c32"])
+    vec(lambda: V.tensor_scalar(T.idn[:], T.row[:], T.pF[:, 0:1], None, ALU.is_equal), ["row", "pF"], ["idn"])
+    vec(lambda: V.tensor_scalar(T.pF[:, 4:5], T.pF[:, 1:2], 16.0, T.pF[:, 3:4], ALU.mult, ALU.add), ["pF"], ["pF4"])
+    vec(lambda: V.tensor_scalar(T.hd[:], T.row[:, 0:8], T.pF[:, 2:3], None, ALU.is_equal), ["row", "pF"], ["hd"])
+    vec(lambda: V.tensor_scalar(T.prm[:], T.permf[:], T.pF[:, 4:5], None, ALU.add), ["permf", "pF4"], ["perm"])
+
+    send(T.vnat[:, own:own + 512], "vn", ["vnat_o"])
+    send(T.znat[:, own:own + 512], "zn", ["znat_o"])
+    op("pool", lambda: g.iota(T.row2[:], [[1, 8], [0, 16]], 0, 0, allow_small_or_imprecise_dtypes=True), (), ["row2"])
+
+    LHS = []
+    for gp in range(2):
+        for a in range(4):
+            o, i = 128 * gp + 32 * a, 32 * a + 16 * gp
+            vec(lambda o=o, i=i: V.tensor_scalar(T.lhs[:, o:o + 32:2], T.axy[:, i:i + 16], 8.0, None, ALU.mult), ["ay"], ["ly%d" % o])
+            act(lambda o=o, i=i: A.activation(T.lhs[:, o + 1:o + 32:2], T.axy[:, 128 + i:128 + i + 16], ACT.Copy), ["ax"], ["lx%d" % o])
+            LHS += ["ly%d" % o, "lx%d" % o]
+
+    def idx_mm(t):
+        kk = 64 if t % 2 == 0 else 96
+        mms = [(T.EB[:, 0:512], T.posL[0:kk, :], T.posR[0:kk, :], True, False)]
+        for blk in range(16):
+            if t < 2:
+                a0 = own + 32 * blk + t
+                zq = T.znat[:, a0:a0 + 31:2]
+            else:
+                a0 = 2048 * (t - 1) + 256 * r + 16 * blk
+                zq = T.zw[:, a0:a0 + 16]
+            for gp in range(2):
+                c0 = 32 * blk + 16 * gp
+                mms.append((T.EB[:, c0:c0 + 16], T.lhs[:, 128 * gp:128 * gp + 128], zq, False, blk == 15 and gp == 1))
+        src = "znat_o" if t < 2 else "zs%d_o" % (t - 1)
+        sync("pe", (), ["EB"], ())
+        pe(mms, POS + LHS + [src], [ps("E")])
+        writer["EB"] = [touch[ps("E")]["pe"]]
+        readers["EB"] = []
+
+    def idx_ops(t):
+        o = T.off[:, 256 * t:256 * t + 256]
+        ops = [lambda: vec(lambda: V.transpose(T.eT[:], T.EB[:]), ["EB"], ["eT"], [ps("E")]),
+               lambda: vec(lambda: V.tensor_copy(T.eI[:], T.eT[:]), ["eT"], ["eI"]),
+               lambda: vec(lambda: V.tensor_scalar(T.yI[:], T.eI[:, 0:512:2], 0x7C0, None, ALU.bitwise_and), ["eI"], ["yI"])]
+        if t == 0:
+            ops += [lambda: vec(lambda: V.tensor_scalar(T.uI[:], T.eI[:, 1:512:2], 3, 127, ALU.arith_shift_right, ALU.bitwise_and), ["eI"], ["uI"]),
+                    lambda: vec(lambda: V.tensor_scalar(T.EB[:, 0:256], T.yI[:], 2.0, None, ALU.mult), ["yI"], ["EB"], [ps("E")]),
+                    lambda: vec(lambda: V.tensor_tensor(T.tI[:], T.EB[:, 0:256], T.uI[:], ALU.add), ["EB", "uI"], ["tI"], [ps("E")])]
+        else:
+            ops += [lambda: vec(lambda: V.tensor_scalar(T.uI[:], T.eI[:, 1:512:2], 0x3F8, None, ALU.bitwise_and), ["eI"], ["uI"]),
+                    lambda: vec(lambda: V.tensor_scalar(T.EB[:, 0:256], T.uI[:], 256.0625, 2048.0 * (t % 2) - 0.25, ALU.mult, ALU.add),
+                                ["uI"], ["EB"], [ps("E")]),
+                    lambda: vec(lambda: V.tensor_tensor(T.sI[:], T.EB[:, 0:256], T.yI[:], ALU.add), ["EB", "yI"], ["sI"], [ps("E")]),
+                    lambda: vec(lambda: V.tensor_scalar(T.tI[:], T.sI[:], 0xFFF, None, ALU.bitwise_and), ["sI"], ["tI"])]
+        ops.append(lambda: vec(lambda: V.tensor_copy(o, T.tI[:, 0:256].indirect(T.prm[:, 0:16])), ["tI", "perm"], ["off%d" % t]))
+        return ops
+
+    def vrep(t):
+        for c in range(2):
+            if t < 2:
+                a0 = own + 256 * c + t
+                src, nm = T.vnat[:, a0:a0 + 255:2], "vnat_o"
+            else:
+                a0 = 2048 * (t - 1) + 256 * r + 128 * c
+                src, nm = T.vw[:, a0:a0 + 128], "vs%d_o%d" % (t - 1, c)
+            for j in range(4):
+                o = 1024 * (t % 2) + 512 * c + 128 * j
+                act(lambda o=o, src=src: A.activation(T.vrep[:, o:o + 128], src, ACT.Copy), [nm], ["vr%d" % o])
+
+    idx_mm(0)
+    for f in idx_ops(0):
+        f()
+    vrep(0)
+    vec(lambda: V.tensor_scalar(T.sal[:], T.row2[:], T.pF[:, 1:2], None, ALU.is_equal), ["row2", "pF"], ["sal"])
+    BIG = []
+    for c in range(16):
+        act(lambda c=c: A.activation(T.big[:, c:2048:16], T.idn[:], ACT.Copy), ["idn"], ["big%d" % c])
+        BIG.append("big%d" % c)
+    op("pool", lambda: g.affine_select(T.zw[:, 0:2048], T.znat[:, 1:4096:2], [[0, 2048]], ALU.is_ge, 0.0, 0, 0),
+       ["znat_o", "znat_r"], ["zs0_o"])
+
+    W = [T.W0, T.W1, T.W2, T.W3]
+    SB, SN = [T.ST, T.W3], [ps("S"), ps("W3")]
+    LNW = -0.25 - math.log(64.0)
+
+    for t in range(R):
+        last = t == R - 1
+        if t == 0:
+            vwin, vnm = T.vnat[:, 0:4096], ["vnat_o", "vnat_r"]
+            zwin, znm = T.znat[:, 0:4096], ["znat_o", "znat_r"]
+        else:
+            vwin, zwin = T.vw[:, 2048 * (t - 1):2048 * (t + 1)], T.zw[:, 2048 * (t - 1):2048 * (t + 1)]
+            vnm = ["vs%d_%s" % (s, x) for s in (t - 1, t) for x in ("o0", "o1", "r")]
+            znm = ["zs%d_%s" % (s, x) for s in (t - 1, t) for x in ("o", "r")]
+        offn = "off%d" % t
+        ob = 256 * t
+        bank = [[0, 1, 2, 3], [1, 2, 3, 0]]
+
+        def dcol(c, b):
+            return 2048 * c + 512 * b
+
+        def gat(c, b):
+            d, vo = dcol(c, b), 1024 * (t % 2) + 512 * c
+            o = ob + 128 * c + 32 * b
+            vec(lambda: V.tensor_tensor(T.dif[:, d:d + 512], vwin.indirect(T.off[:, o:o + 32]), T.vrep[:, vo:vo + 512], ALU.subtract),
+                vnm + [offn] + ["vr%d" % (vo + 128 * j) for j in range(4)], ["d%d" % d])
+
+        def absb(c, b):
+            d = dcol(c, b)
+            act(lambda: A.activation(T.ab[:, d:d + 512], T.dif[:, d:d + 512], ACT.Abs), ["d%d" % d], ["a%d" % d])
+
+        def smm(c, b):
+            d = dcol(c, b)
+            pe([(SB[c][:, 8 * (4 * b + j):8 * (4 * b + j) + 8], T.ab[:, d + 128 * j:d + 128 * j + 128], T.hd[:], True, True)
+                for j in range(4)], ["a%d" % d, "hd"], [SN[c]])
+
+        def relu(c):
+            act(lambda: A.activation(T.rT[:, 128 * c:128 * c + 128], SB[c][:, 0:128], ACT.Relu, bias=0.25, scale=-1.0 / 128),
+                (), ["rT%d" % c], [SN[c]])
+
+        def turn(c):
+            op("pe", lambda: P.transpose(T.RB[:, 0:128], T.rT[:, 128 * c:128 * c + 128], T.idn[:]), ["rT%d" % c, "idn"], (), [ps("R")])
+
+        def expo(c):
+            act(lambda: A.activation(T.RB[:, 128:256], T.RB[:, 0:128], ACT.Exp, bias=LNW, scale=1.0), (), ["wf"], [ps("R")])
+            act(lambda: A.activation(T.whi[:, 128 * c:128 * c + 128], T.RB[:, 0:128], ACT.Exp, bias=LNW, scale=1.0), (), ["hi%d" % c], [ps("R")])
+
+        def low(c):
+            vec(lambda: V.tensor_tensor(T.wlo[:, 128 * c:128 * c + 128], T.RB[:, 128:256], T.whi[:, 128 * c:128 * c + 128], ALU.subtract),
+                ["wf", "hi%d" % c], ["lo%d" % c], [ps("R")])
+
+        def spread(c, b):
+            w = bank[c][b]
+            mms = []
+            for j in range(4):
+                k = 4 * b + j
+                mms.append((W[w][:, 128 * j:128 * j + 128], T.big[:, 128 * k:128 * k + 128], T.whi[:, 128 * c:128 * c + 128], True, False))
+                mms.append((W[w][:, 128 * j:128 * j + 128], T.big[:, 128 * k:128 * k + 128], T.wlo[:, 128 * c:128 * c + 128], False, True))
+            pe(mms, BIG + ["hi%d" % c, "lo%d" % c], [ps("W%d" % w)])
+
+        def sumw(c):
+            o = T.FB[:, 256 + 128 * c:384 + 128 * c]
+            pe([(o, T.sal[:], T.whi[:, 128 * c:128 * c + 128], True, False), (o, T.sal[:], T.wlo[:, 128 * c:128 * c + 128], False, False),
+                (o, T.sal[:], T.c32[:], False, True)], ["sal", "c32", "hi%d" % c, "lo%d" % c], [ps("F")])
+
+        def tterm(c):
+            vo = 1024 * (t % 2) + 512 * c
+            vec(lambda: V.tensor_tensor(T.tq[:, 128 * c:128 * c + 128], T.FB[:, 256 + 128 * c:384 + 128 * c], T.vrep[:, vo:vo + 128], ALU.mult),
+                ["vr%d" % vo], ["tq%d" % c], [ps("F")])
+
+        def mul(c, b, keep):
+            d, w = dcol(c, b), bank[c][b]
+            if keep:
+                vec(lambda: V.tensor_tensor(W[w][:], W[w][:], T.dif[:, d:d + 512], ALU.mult), ["d%d" % d], ["Wv%d" % w], [ps("W%d" % w)])
+            else:
+                vec(lambda: V.tensor_tensor(T.dif[:, d:d + 512], W[w][:], T.dif[:, d:d + 512], ALU.mult), (), ["d%d" % d], [ps("W%d" % w)])
+
+        def add(c, bw, b, keep):
+            d, w = dcol(c, b), bank[c][bw]
+            if keep:
+                vec(lambda: V.tensor_tensor(W[w][:], W[w][:], T.dif[:, d:d + 512], ALU.add), ["d%d" % d], ["Wv%d" % w], [ps("W%d" % w)])
+            else:
+                vec(lambda: V.tensor_tensor(T.dif[:, d:d + 512], W[w][:], T.dif[:, d:d + 512], ALU.add), ["Wv%d" % w], ["d%d" % d], [ps("W%d" % w)])
+
+        def fold(c, b, first, end):
+            d = dcol(c, b)
+            pe([(T.FB[:, 128 * c:128 * c + 128], T.idn[:], T.dif[:, d + 128 * j:d + 128 * j + 128], first and j == 0, end and j == 3)
+                for j in range(4)], ["d%d" % d, "idn"], [ps("F")])
+
+        def fin(c):
+            if last:
+                o, nm = T.ovb[:, 256 * c:256 * c + 256:2], "ove%d" % c
+            else:
+                a0 = 2048 * (t + 1) + 256 * r + 128 * c
+                o, nm = T.vw[:, a0:a0 + 128], "vs%d_o%d" % (t + 1, c)
+            vec(lambda: V.tensor_tensor(o, T.FB[:, 128 * c:128 * c + 128], T.tq[:, 128 * c:128 * c + 128], ALU.add),
+                ["tq%d" % c], [nm], [ps("F")])
+            if last:
+                dma("sp", "st%d" % c, T.yv[:, 256 * c:256 * c + 256], T.ovb[:, 256 * c:256 * c + 256], [nm, "ovo"], ())
+            else:
+                send(o, "av%d" % t, [nm])
+
+        zn = [0]
+
+        def zgat(n):
+            for _ in range(n):
+                c, k = divmod(zn[0], 16)
+                zn[0] += 1
+                o = ob + 128 * c + 8 * k
+                act(lambda: A.activation(T.zg[:, 2048 * c + k:2048 * c + 2048:16], zwin.indirect(T.off[:, o:o + 8]), ACT.Copy),
+                    znm + [offn], ["zg%d_%d" % (c, k)])
+
+        def scan(c):
+            vec(lambda: V.tensor_tensor_scan(T.zs[:, 2048 * c:2048 * c + 2048], T.msk[:], T.zg[:, 2048 * c:2048 * c + 2048], 0.0, ALU.mult, ALU.max),
+                ["msk"] + ["zg%d_%d" % (c, k) for k in range(16)], ["zm%d" % c])
+
+        def mix():
+            pe([(T.ST[:, 256:512], T.bms[:], T.zs[:, 15:4096:16], True, True)], ["bm", "zm0", "zm1"], [ps("S")])
+
+        def zu1():
+            vec(lambda: V.tensor_copy(T.bI[:], T.ST[:, 256:512]), (), ["bI"], [ps("S")])
+
+        def zu2():
+            vec(lambda: V.tensor_scalar(T.cI[:], T.bI[:], 2, 15, ALU.arith_shift_right, ALU.bitwise_and), ["bI"], ["cI"])
+
+        def zu3():
+            if last:
+                vec(lambda: V.tensor_copy(T.ozb[:, 0:512:2], T.cI[:]), ["cI"], ["oze"])
+                dma("act", "st2", T.yz[:], T.ozb[:], ["oze", "ozo"], ())
+            else:
+                a0 = 2048 * (t + 1) + 256 * r
+                vec(lambda: V.tensor_copy(T.zw[:, a0:a0 + 256], T.cI[:]), ["cI"], ["zs%d_o" % (t + 1)])
+                send(T.zw[:, a0:a0 + 256], "az%d" % t, ["zs%d_o" % (t + 1)])
+
+        ix = []
+        if not last:
+            idx_mm(t + 1)
+            ix = idx_ops(t + 1)
+
+        def nxt(n):
+            for _ in range(n):
+                if ix:
+                    ix.pop(0)()
+
+        for b in range(4):
+            gat(0, b); absb(0, b); smm(0, b)
+        gat(1, 0); absb(1, 0); relu(0); turn(0); smm(1, 0)
+        gat(1, 1); absb(1, 1); smm(1, 1); expo(0)
+        gat(1, 2); low(0); spread(0, 0); absb(1, 2); smm(1, 2)
+        gat(1, 3); spread(0, 1); sumw(0); absb(1, 3); zgat(2); smm(1, 3)
+        mul(0, 0, True); mul(0, 1, False); tterm(0)
+        spread(0, 2); relu(1); turn(1); spread(0, 3); zgat(1); expo(1)
+        add(0, 0, 1, True); mul(0, 2, False); low(1)
+        zgat(29)
+        sumw(1); spread(1, 0); spread(1, 1)
+        add(0, 0, 2, True); mul(0, 3, False); spread(1, 2); tterm(1); add(0, 0, 3, False)
+        fold(0, 3, True, True); spread(1, 3)
+        mul(1, 0, True); mul(1, 1, False); fin(0); add(1, 0, 1, False)
+        fold(1, 1, True, False)
+        mul(1, 2, True); mul(1, 3, False); add(1, 2, 3, False)
+        fold(1, 3, False, True)
+        if last:
+            scan(0); fin(1); scan(1); mix(); zu1(); zu2(); zu3()
+        else:
+            nxt(2); fin(1)
+            if t == 0:
+                act(lambda: A.activation(T.vw[:, 0:2048], T.vnat[:, 1:4096:2], ACT.Copy), ["vnat_o", "vnat_r"], ["vs0_o0"])
+            vrep(t + 1)
+            scan(0); nxt(2); scan(1); mix(); nxt(2); zu1(); nxt(1); zu2(); nxt(1); zu3()
+            if t == R - 2:
+                a0 = 2048 * (t + 1) + 256 * r
+                act(lambda: A.activation(T.ovb[:, 1:512:2], T.vw[:, a0:a0 + 256], ACT.Copy), ["vs%d_o0" % (t + 1), "vs%d_o1" % (t + 1)], ["ovo"])
+                act(lambda: A.activation(T.ozb[:, 1:512:2], T.zw[:, a0:a0 + 256], ACT.Copy), ["zs%d_o" % (t + 1)], ["ozo"])
+
+    for s in ("pe", "dve", "act", "pool", "sent"):
+        g.wait_ge(T.sem[s], cnt[s])
+    for s in ("st0", "st1", "st2"):
+        g.wait_ge(T.sem[s], 16)

@@ -4,6 +4,46 @@ from concourse.mybir import AluOpType as ALU, ActivationFunctionType as ACT
 
 R = 5
 NR = 8
+UNITS = [(0, 2), (2, 2), (4, 2), (6, 2)]
+GROUPS = [(0, 4), (4, 4)]
+RAW = [[], [], [], [], []]
+FINE = [0, 1, 2, 3]
+ZG, ZS = 2, 4
+ZV = [[6, 7], [6, 7], [6, 7], [6, 7], [7]]
+NG = len(GROUPS)
+NW = 2
+CYC, PEC, GATH = 0.9, 0.46, 1.56
+FIX = {"dve": 55.0, "act": 70.0, "pe": 0.0, "pool": 170.0}
+HOP, LOAD, ISSUE, FIRST, LAND = 100.0, 2400.0, 400.0, 2000.0, 1600.0
+ROW, RATE = 25.0, 20.0
+QUEUES = {
+    "dve": "g00 g01 g02 g03 g11 g10 g12 g13 g20 g21 g22 g23 lo0 g31 g32 g30 h0 lo1 h1 g33 h2 h3 tq0 fw0 lo2 fin0 h4 lo3 h5 h6 h7 tq1 fw1 fin1 "
+           "zg7 zg6 zm1 zm2 zm0 zm3 off+ bI cI zo",
+    "act": "a00 a01 a02 a03 kilo+ a11 a10 a12 rp0 a13 a20 hi0 wf0 a21 a22 rp1 a23 ew0 hi1 wf1 a30 a32 a31 rp2 us0 a33 hi2 wf2 zg1 rp3 ew1 hi3 wf3 "
+           "zg0 us1 zg2 zg3 zg4 zg5 fh+ fy+ fx+",
+    "pe": "mm+ s1 s0 rd0 s2 s3 w1 w0 rd1 s4 u0 s5 w2 w3 rd2 f0 s7 s6 w4 rd3 w5 u1 w6 w7 f1 mod+ sum+ mix",
+    "pool": "ov0 ov1 ov2 ov3 vr0+ vr1+ vr2+ vr3+ send0 send1 oz0 oz1 oz2 sendz oz3",
+}
+LAST = {
+    "dve": "g02 g00 g01 g03 g10 g12 g11 g13 g21 g20 g22 g31 g23 g32 g33 g30 lo0 zg7 h1 lo1 h0 h3 lo2 h2 h5 h4 fw0 tq0 lo3 zm0 zm1 h7 h6 zm3 zm2 "
+           "tq1 fw1 bI fin0 cI fin1 zo",
+    "act": "ovo a02 a00 a01 a03 a10 ozo a12 a11 rp0 a13 a21 a20 wf0 a22 a31 rp1 a23 hi0 a32 a33 wf1 a30 ew0 hi1 rp2 zg1 zg2 hi2 wf2 rp3 zg3 us0 wf3 hi3 "
+           "zg0 zg6 zg4 ew1 zg5 us1",
+    "pe": "s1 s0 rd0 s2 s3 rd1 s5 s4 w1 w0 s6 rd2 u0 w3 s7 w2 w5 rd3 w4 f0 w6 w7 u1 f1 mix",
+    "sp": "st0 st1 stz",
+}
+
+
+def keys(steps, group):
+    key, out = {}, []
+    for t in range(R):
+        for q, names in (LAST if t == R - 1 else QUEUES).items():
+            for i, x in enumerate(names.split()):
+                key[q, x.strip("+-"), t + x.count("+") - x.count("-")] = 1000 * t + i
+    for i, (x, t) in enumerate(group):
+        out.append(out[-1] if steps[i][0] == "wire" else i - 10000 if x is None else key[steps[i][0], x, t])
+    return out
+
 
 SCRATCH = {
     "vnat": ("sbuf", [128, 4096], "bfloat16"),
@@ -12,52 +52,86 @@ SCRATCH = {
     "zw": ("sbuf", [128, 5 * 2048], "bfloat16"),
     "dif": ("sbuf", [128, 4096], "float32"),
     "ab": ("sbuf", [128, 4096], "float32"),
+    "hs": ("sbuf", [128, 4096], "float32"),
     "zg": ("sbuf", [128, 4096], "bfloat16"),
     "zs": ("sbuf", [128, 4096], "bfloat16"),
-    "msk": ("sbuf", [128, 2048], "bfloat16"),
-    "vrep": ("sbuf", [128, 2048], "float32"),
+    "msk": ("sbuf", [128, 4096 // ZS], "bfloat16"),
+    "vq4": ("sbuf", [128, 2048], "float32"),
     "off": ("sbuf", [128, 5 * 256], "uint16"),
-    "prm": ("sbuf", [128, 16], "uint16"),
-    "permf": ("sbuf", [128, 16], "float32"),
-    "eT": ("sbuf", [128, 512], "float32"),
-    "eI": ("sbuf", [128, 512], "int32"),
-    "yI": ("sbuf", [128, 256], "int32"),
-    "uI": ("sbuf", [128, 256], "int32"),
-    "sI": ("sbuf", [128, 256], "int32"),
-    "tI": ("sbuf", [128, 256], "int32"),
+    "fld": ("sbuf", [128, 1280], "bfloat16"),
+    "dg": ("sbuf", [128, 512], "bfloat16"),
     "bI": ("sbuf", [128, 256], "int32"),
     "cI": ("sbuf", [128, 256], "int32"),
     "pI": ("sbuf", [128, 8], "int32"),
     "pF": ("sbuf", [128, 8], "float32"),
     "row": ("sbuf", [128, 128], "float32"),
-    "row2": ("sbuf", [128, 128], "float32"),
     "idn": ("sbuf", [128, 128], "float32"),
-    "hd": ("sbuf", [128, 8], "float32"),
-    "big": ("sbuf", [128, 2048], "bfloat16"),
-    "sal": ("sbuf", [128, 128], "bfloat16"),
-    "c32": ("sbuf", [128, 128], "bfloat16"),
+    "nid": ("sbuf", [128, 128], "float32"),
+    "dm": ("sbuf", [128, 128], "float32"),
+    "j2": ("sbuf", [128, 64], "float32"),
+    "r16": ("sbuf", [128, 32], "float32"),
+    "hd2": ("sbuf", [128, 16], "float32"),
+    "wide": ("sbuf", [128, 128], "float32"),
+    "big": ("sbuf", [128, 1024], "bfloat16"),
+    "cb": ("sbuf", [128, 256], "bfloat16"),
     "posL": ("sbuf", [128, 128], "bfloat16"),
     "posR": ("sbuf", [128, 512], "bfloat16"),
     "axy": ("sbuf", [128, 256], "bfloat16"),
     "bms": ("sbuf", [128, 128], "bfloat16"),
-    "lhs": ("sbuf", [128, 256], "bfloat16"),
-    "rT": ("sbuf", [128, 256], "float32"),
-    "whi": ("sbuf", [128, 256], "bfloat16"),
-    "wlo": ("sbuf", [128, 256], "bfloat16"),
+    "mk": ("sbuf", [128, 288], "bfloat16"),
+    "lhs": ("sbuf", [128, 16 + 8 * 144], "bfloat16"),
+    "rp": ("sbuf", [128, 512], "float32"),
+    "ew": ("sbuf", [128, 256], "float32"),
+    "us": ("sbuf", [128, 512], "float32"),
+    "whi": ("sbuf", [128, 512], "bfloat16"),
+    "wlo": ("sbuf", [128, 512], "float16"),
     "tq": ("sbuf", [128, 256], "float32"),
     "ovb": ("sbuf", [128, 512], "float32"),
     "ozb": ("sbuf", [128, 512], "float32"),
     "W0": ("psum", [128, 512], "float32"),
     "W1": ("psum", [128, 512], "float32"),
-    "W2": ("psum", [128, 512], "float32"),
-    "W3": ("psum", [128, 512], "float32"),
-    "ST": ("psum", [128, 512], "float32"),
-    "RB": ("psum", [128, 512], "float32"),
+    "S0": ("psum", [128, 512], "float32"),
+    "S1": ("psum", [128, 512], "float32"),
+    "R0": ("psum", [128, 512], "float32"),
+    "R1": ("psum", [128, 512], "float32"),
     "FB": ("psum", [128, 512], "float32"),
     "EB": ("psum", [128, 512], "float32"),
 }
-SEMAPHORES = (["pe", "dve", "act", "pool", "sent", "ldv", "ldz", "ldy", "ldx", "ldb", "st0", "st1", "st2", "vn", "zn"]
-              + ["av%d" % i for i in range(4)] + ["az%d" % i for i in range(4)])
+SEMAPHORES = (["pe", "dve", "act", "pool", "sent", "ldv", "ldz", "ldy", "ldx", "ldb", "stz", "vn", "zn"]
+              + ["st%d" % i for i in range(NG)] + ["av%d" % i for i in range(4)] + ["az%d" % i for i in range(4)])
+ORDER = []
+
+
+def schedule(steps, key):
+    n = len(steps)
+    preds, writer, readers = [], {}, {}
+    for i, (q, d, lag, reads, writes, banks) in enumerate(steps):
+        p = set()
+        for x in reads:
+            p.update(writer[x])
+        for x in writes:
+            if not x.endswith("_r"):
+                p.update(writer.get(x, []) + readers.get(x, []))
+        preds.append(p)
+        for x in reads:
+            readers.setdefault(x, []).append(i)
+        for x in writes:
+            writer[x] = (writer.get(x, []) if x.endswith("_r") else []) + [i]
+            readers[x] = []
+    queues = {}
+    for i in sorted(range(n), key=lambda k: (key[k], k)):
+        queues.setdefault(steps[i][0], []).append(i)
+    free, done, bank, order = {q: 0.0 for q in queues}, {}, {}, []
+    while len(order) < n:
+        heads = [l[0] for l in queues.values() if l and all(p in done for p in preds[l[0]])]
+        t, i = min((max([free[steps[k][0]]] + [done[p] for p in preds[k]]
+                        + [e for b in steps[k][5] for o, e in bank.get(b, {}).items() if o != steps[k][0]]), k) for k in heads)
+        q, d, lag = steps[i][:3]
+        order.append(queues[q].pop(0))
+        free[q], done[i] = t + d, t + d + lag
+        for b in steps[i][5]:
+            bank.setdefault(b, {})[q] = t + d + HOP
+    return order
 
 
 def rank_program(g, core, T, topo):
@@ -66,14 +140,368 @@ def rank_program(g, core, T, topo):
         return
     Q = {"pe": g.tensor, "dve": g.vector, "act": g.scalar, "pool": g, "sp": g.sync}
     V, A, P = g.vector, g.scalar, g.tensor
+    steps, calls, group, names = [], [], [], []
+
+    peers = [T.cores[(r + j) % NR] for j in range(1, NR)]
+    emask = topo.mask(core, peers[0])
+    for c in peers[1:]:
+        emask &= topo.mask(core, c)
+    neng = bin(emask).count("1")
+    ids = [DstId(rid=topo.addr(c)[0], pnc=topo.addr(c)[1]) for c in peers]
+
+    def step(s, call):
+        steps.append(s)
+        calls.append(call)
+        group.append(names.pop(0) if names and s[0] != "wire" else (None, 0))
+
+    def name(t, text):
+        names.extend((x, t) for x in text.split())
+
+    def op(q, cycles, fn, args, reads, writes, banks, kw=None):
+        step((q, FIX[q] + max(cycles, 64) * (PEC if q == "pe" else CYC), HOP, list(reads), list(writes), list(banks)), ("op", fn, args, kw or {}))
+
+    def vec(cycles, fn, args, reads=(), writes=(), banks=()):
+        op("dve", cycles, fn, args, reads, writes, banks)
+
+    def act(cycles, out, in_, func, reads=(), writes=(), banks=(), **kw):
+        op("act", cycles, A.activation, (out, in_, func), reads, writes, banks, kw)
+
+    def pool(n, fn, args, reads=(), writes=(), **kw):
+        op("pool", 2 * n, fn, args, reads, writes, (), kw)
+
+    def matmuls(mms):
+        return [P.matmul(*m) for m in mms][-1]
+
+    def pe(cycles, mms, reads=(), writes=(), banks=()):
+        op("pe", cycles, matmuls, (mms,), reads, writes, banks)
+
+    def dma(q, sem, out, in_, reads=(), writes=()):
+        step((q, 60.0, LOAD, list(reads), list(writes), []), ("dma", sem, out, in_))
+
+    nsent = [0]
+
+    def send(ap, nbytes, sem, reads, arrival):
+        nsent[0] += 1
+        step(("pool", ISSUE, FIRST if nsent[0] == 1 else 0.0, list(reads), ["issue%d" % nsent[0]], []), ("send", ap, sem))
+        step(("wire", 128 * (NR - 1) / neng * (ROW + nbytes / RATE), LAND, ["issue%d" % nsent[0]], [arrival], []), ("wire", sem, arrival))
+
+    def iota(n, out, pattern, base, cm, reads, writes):
+        pool(n, g.iota, (out, pattern, base, cm), reads, writes, allow_small_or_imprecise_dtypes=True)
+
+    def fill(n, ap, value, reads, writes):
+        vec(n, V.memset, (ap, value), reads, writes)
+
+    def equal(n, out, in_, col, writes):
+        vec(n, V.tensor_scalar, (out, in_, T.pF[:, col:col + 1], None, ALU.is_equal), ["row", "pF", "pF2"], writes)
+
+    def const(n, out, like, value, writes):
+        act(n, out, like, ACT.Identity, ["znat_o"], writes, scale=0.0, bias=value)
+
+    def vslot(s):
+        return ["vs0_%d" % i for i in range(4)] if s == 0 else ["vs%d_r" % s] + ["vs%d_o%d" % (s, c) for c in range(NG)]
+
+    def zslot(s):
+        return ["zs0_%d" % i for i in range(4)] if s == 0 else ["zs%d_r" % s, "zs%d_o" % s]
+
+    own = 512 * r
+    POS = ["posRy", "posRx", "posR1", "posR2", "posL0", "posL1", "posL2"]
+    LHS = ["lhs%d" % i for i in range(8)]
+    MK = ["mk%d" % i for i in range(8)]
+    BIG = ["big%d" % c for c in range(16)]
+    US = ["us%d" % c for c in range(NG)]
+    DG = ["dg%d" % i for i in range(4)]
+    BASE = 1.5 * 2 ** 17
+
+    def offsets(t, part):
+        E, en, ed = T.EB, "E", ["EB"]
+        kk = 64 if t % 2 == 0 else 96
+        mms = [(E[:, 0:512], T.posL[0:kk, :], T.posR[0:kk, :], True, False)]
+        for i in range(8):
+            for ql in range(4):
+                if t < 2:
+                    zq = T.znat[:, own + 2 * ql + t:own + 512:8]
+                else:
+                    a0 = 2048 * (t - 1) + 256 * r
+                    zq = T.zw[:, a0 + ql:a0 + 256:4]
+                o = 16 + 144 * i + 4 * (i % 4 - ql)
+                mms.append((E[:, 64 * i:64 * i + 64], T.lhs[:, o:o + 128], zq, False, False))
+        src = POS + LHS + ["znat_o" if t < 2 else "zs%d_o" % (t - 1)]
+        if part == 0:
+            if t > 0:
+                name(t, "mm")
+            return pe(2560, mms[:-1] + [mms[-1][:4] + (True,)], src, ed, [en])
+        if t > 0:
+            name(t, "kilo mod fy fx fh sum off")
+
+        def floor(out, src, unit, scale, nm):
+            act(256, out, src, ACT.Identity, ed, [nm], [en], scale=scale, bias=scale * (BASE + 129 * unit - unit / 2 + 0.5))
+            return scale * 129 * unit
+
+        one, minus, up, down = [T.dg[:, 128 * i:128 * i + 128] for i in range(4)]
+        fy, fx, fh = T.fld[:, 512:768], T.fld[:, 768:1024], T.fld[:, 1024:1280]
+        act(512, T.fld[:, 0:512], E[:], ACT.Identity, ed, ["kilo"], [en], bias=BASE - 511.5)
+        pe(3072, mms + [(E[:], minus, T.fld[:, 0:512], False, True)], ["kilo", "dg1"] + src, ed, [en])
+        if t == 0:
+            c = floor(fy, E[:, 0:256], 32, 4.0, "fy") + floor(fx, E[:, 256:512], 8, 0.125, "fx")
+            terms, nm = [(one, fy), (one, fx)], ["fy", "fx"]
+        else:
+            cy, cx, ch = floor(fy, E[:, 0:256], 32, 2.0, "fy"), floor(fx, E[:, 256:512], 8, 256.0, "fx"), floor(fh, E[:, 256:512], 16, 0.0625, "fh")
+            sg = 1 - 2 * (t % 2)
+            c = cy + ch + sg * (cx - 4096 * ch) - 2048 * (t % 2)
+            terms, nm = [(one, fy), (one, fh), (minus if t % 2 else one, fx), (up if t % 2 else down, fh)], ["fy", "fx", "fh"]
+        pe(256 * len(terms), [(E[:, 0:256], a, b, i == 0, i == len(terms) - 1) for i, (a, b) in enumerate(terms)], nm + DG, ed, [en])
+        vec(256, V.tensor_scalar, (T.off[:, 256 * t:256 * t + 256], E[:, 0:256], -c, None, ALU.add), ed, ["off%d" % t], [en])
+
+    def repeat(t):
+        if t < 2:
+            src, nm = T.vnat[:, own + t:own + 512:2], ["vnat_o"]
+        else:
+            a0 = 2048 * (t - 1) + 256 * r
+            src, nm = T.vw[:, a0:a0 + 256], vslot(t - 1)[1:]
+            name(t, "vr0 vr1 vr2 vr3")
+        for j in range(4):
+            o = T.vq4[:, 1024 * (t % 2) + j:1024 * (t % 2) + 1024:4]
+            if t < 2:
+                act(256, o, src, ACT.Copy, nm, ["vr%d_%d" % (t % 2, j)])
+            else:
+                pool(256, g.affine_select, (o, src, [[0, 256]], ALU.is_ge, 0.0, 0, 0), nm, ["vr%d_%d" % (t % 2, j)])
+
+    def odd(dst, src, nm):
+        for i in range(4):
+            name(0, "o%s%d" % (nm, i))
+            pool(512, g.affine_select, (dst[:, 512 * i:512 * i + 512], src[:, 1024 * i + 1:1024 * i + 1024:2], [[0, 512]], ALU.is_ge, 0.0, 0, 0),
+                 [nm + "nat_o", nm + "nat_r"], [nm + "s0_%d" % i])
+
+    dma("sp", "ldv", T.vnat[:, own:own + 512], T.v0[:], (), ["vnat_o"])
+    dma("act", "ldz", T.znat[:, own:own + 512], T.z0[:], (), ["znat_o"])
+    dma("sp", "ldy", T.axy[:, 0:128], T.ay[:], (), ["ay"])
+    dma("act", "ldx", T.axy[:, 128:256], T.ax[:], (), ["ax"])
+    dma("sp", "ldb", T.bms[:], T.bm[:], (), ["bm"])
+    fill(256, T.posR[:], 0.0, (), ["posR"])
+    fill(64, T.posL[:], 0.0, (), ["posL"])
+    pool(1, g.iota, (T.pI[:, 0:1], [[0, 1]], 0, 1), (), ["p0"])
+    iota(128, T.row[:], [[1, 128]], 0, 0, (), ["row"])
+    iota(256, T.posR[0:1, 0:256], [[0, 4], [32, 4], [0, 16]], 128 * r, 0, ["posR"], ["posRy"])
+    iota(256, T.posR[0:1, 256:512], [[0, 16], [64, 16]], 0, 0, ["posR"], ["posRx"])
+    iota(128, T.posL[32:33, :], [[0, 8], [16, 4], [0, 4]], 0, 0, ["posL"], ["posL1"])
+    send(T.vnat[:, own:own + 512], 1024, "vn", ["vnat_o"], "vnat_r")
+    send(T.znat[:, own:own + 512], 1024, "zn", ["znat_o"], "znat_r")
+    iota(128, T.wide[:], [[1, 8], [0, 16]], 0, 0, (), ["wide"])
+    act(1600, T.cb[0:1, 0:128], T.row[0:1, :], ACT.Exp, ["row"], ["cb0"], scale=0.0)
+    repeat(0)
+    fill(144, T.mk[:], 0.0, (), ["mk"])
+    fill(600, T.lhs[:], 0.0, (), ["lhs"])
+    for j in range(4):
+        fill(9, T.mk[:, 12 + j:144:16], 4.0, ["mk"], [MK[j]])
+        fill(9, T.mk[:, 156 + j:288:16], 1.0, ["mk"], [MK[4 + j]])
+    fill(128, T.posR[32:33, 256:512], 1.0, ["posR"], ["posR1"])
+    fill(128, T.posR[64:65, 256:512], 1.0, ["posR"], ["posR2"])
+    fill(64, T.posL[0:1, :], 1.0, ["posL"], ["posL0"])
+    fill(64, T.posL[64:65, :], 8.0, ["posL"], ["posL2"])
+    vec(1, V.tensor_scalar, (T.pI[:, 1:2], T.pI[:, 0:1], 4, None, ALU.arith_shift_right), ["p0"], ["p1"])
+    vec(1, V.tensor_scalar, (T.pI[:, 2:3], T.pI[:, 0:1], 1, None, ALU.arith_shift_right), ["p0"], ["p2"])
+    vec(1, V.tensor_scalar, (T.pI[:, 3:4], T.pI[:, 0:1], 1, None, ALU.bitwise_and), ["p0"], ["p3"])
+    vec(1, V.tensor_copy, (T.pF[:, 0:4], T.pI[:, 0:4]), ["p0", "p1", "p2", "p3"], ["pF"])
+    for h in range(2):
+        for kb in range(4):
+            o, m = 16 + 144 * (4 * h + kb), 144 * h + 12 - 4 * kb
+            vec(128, V.tensor_tensor, (T.lhs[:, o:o + 128], T.axy[:, 128 * h:128 * h + 128], T.mk[:, m:m + 128], ALU.mult),
+                ["lhs", "ay" if h == 0 else "ax"] + MK, [LHS[4 * h + kb]])
+    for i, x in enumerate((1.0, -1.0, 4096.0, -4096.0)):
+        vec(128, V.tensor_scalar, (T.dg[:, 128 * i:128 * i + 128], T.row[:], T.pF[:, 0:1], x, ALU.is_equal, ALU.mult), ["row", "pF"], [DG[i]])
+    vec(1, V.tensor_scalar, (T.pF[:, 4:5], T.pF[:, 0:1], 1.0, None, ALU.add), ["pF"], ["pF2"])
+    vec(1, V.tensor_scalar, (T.pF[:, 5:6], T.pF[:, 3:4], 128.0, -128.0, ALU.mult, ALU.add), ["pF"], ["pF5"])
+    vec(1, V.tensor_scalar, (T.pF[:, 6:7], T.pF[:, 3:4], 2.0, -1.0, ALU.mult, ALU.add), ["pF"], ["pF6"])
+    equal(128, T.idn[:], T.row[:], 0, ["idn"])
+    equal(128, T.dm[:], T.row[:], 4, ["dm"])
+    equal(128, T.wide[:], T.wide[:], 0, ["wide"])
+    vec(64, V.tensor_scalar, (T.j2[:], T.row[:, 0:64], T.pF[:, 2:3], T.pF[:, 6:7], ALU.is_equal, ALU.mult), ["row", "pF", "pF6"], ["j2"])
+    equal(8, T.hd2[:, 0:16:2], T.row[:, 0:8], 1, ["hd2a"])
+    equal(8, T.hd2[:, 1:16:2], T.row[:, 0:8], 1, ["hd2b"])
+    equal(8, T.r16[:, 0:16:2], T.row[:, 0:8], 1, ["r16a"])
+    equal(8, T.r16[:, 1:16:2], T.row[:, 15:128:16], 0, ["r16b"])
+    fill(128, T.wide[32:33, :], 1.0, (), ["wide"])
+    vec(256, V.tensor_tensor, (T.dm[:], T.dm[:], T.idn[:], ALU.subtract), ["idn"], ["dm"])
+    fill(64, T.cb[0:1, 128:256], 0.0, (), ["cb1"])
+    fill(512, T.us[0:64, :], 0.0, (), US)
+    fill(2048 // ZS, T.msk[:], 1.0, (), ["msk"])
+    fill(8, T.cb[0:1, 128:256:16], -128.0, (), ["cb1"])
+    fill(256, T.us[32:33, 0:512:2], 0.5, (), US)
+    fill(256 // ZS, T.msk[:, 0:4096 // ZS:16], 0.0, (), ["msk"])
+    repeat(1)
+    offsets(0, 0)
+    offsets(0, 1)
+    for c in range(16):
+        if c % 2:
+            vec(64, V.tensor_copy, (T.big[:, c:1024:16], T.j2[:]), ["j2"], [BIG[c]])
+        else:
+            act(64, T.big[:, c:1024:16], T.j2[:], ACT.Copy, ["j2"], [BIG[c]])
+    R16 = ["r16a", "r16b"]
+    if any(RAW):
+        act(8, T.r16[:, 17:32:2], T.idn[:, 15:128:16], ACT.Copy, ["idn"], ["r16d"])
+        const(8, T.r16[:, 16:32:2], T.znat[:, own:own + 8], 0.0, ["r16c"])
+        act(128, T.nid[:], T.idn[:], ACT.Copy, ["idn"], ["nid"], scale=-1.0)
+        R16 += ["r16c", "r16d"]
+
+    W = [T.W0, T.W1]
+    SB = [T.S0, T.S1]
+    LNW = -0.25 - math.log(64.0)
+    nbank = [0]
+
+    def bank():
+        nbank[0] += 1
+        return nbank[0] % NW, "W%d" % (nbank[0] % NW)
+
+    def v_layer(t):
+        last = t == R - 1
+        ob, vo = 256 * t, 1024 * (t % 2)
+        if t == 0:
+            vwin, vnm = T.vnat[:, 0:4096], ["vnat_o", "vnat_r"]
+        else:
+            vwin, vnm = T.vw[:, 2048 * (t - 1):2048 * (t + 1)], vslot(t - 1) + vslot(t)
+        VR = ["vr%d_%d" % (t % 2, j) for j in range(4)]
+        D = [["d%d_%d" % (b, kb) for kb in range(4)] for b in range(8)]
+        AB = [["a%d_%d" % (b, kb) for kb in range(4)] for b in range(8)]
+        raw = [b for u in RAW[t] for b in range(UNITS[u][0], sum(UNITS[u]))]
+        if last:
+            a0 = 2048 * t + 256 * r
+            name(t, "ovo")
+            act(256, T.ovb[:, 1:512:2], T.vw[:, a0:a0 + 256], ACT.Copy, vslot(t)[1:], ["ovo"])
+
+        for u, (b, n) in enumerate(UNITS):
+            for kb in range(4):
+                d, src = slice(512 * b + kb, 512 * (b + n), 4), vwin.indirect(T.off[:, ob + 64 * kb + 8 * b:ob + 64 * kb + 8 * (b + n)])
+                nm = [D[x][kb] for x in range(b, b + n)]
+                name(t, "g%d%d" % (u, kb))
+                if b in raw:
+                    act(128 * n * GATH, T.dif[:, d], src, ACT.Copy, vnm + ["off%d" % t], nm)
+                else:
+                    vec(128 * n * GATH, V.tensor_tensor, (T.dif[:, d], src, T.vq4[:, vo + 128 * b:vo + 128 * (b + n)], ALU.subtract),
+                        vnm + ["off%d" % t] + VR, nm)
+                    if u in FINE:
+                        name(t, "a%d%d" % (u, kb))
+                        act(128 * n, T.ab[:, d], T.dif[:, d], ACT.Abs, nm, [AB[x][kb] for x in range(b, b + n)])
+            for x in range(b, b + n):
+                d = slice(512 * x, 512 * x + 512)
+                if x in raw:
+                    w, wn = bank()
+                    name(t, "pre%d sub%d a%d" % (x, x, x))
+                    pe(2048, [(W[w][:, kb:512:4], T.nid[:], T.vq4[:, vo + 128 * x:vo + 128 * x + 128], kb == 0, False) for kb in range(4)],
+                       VR + ["nid"], [wn + "d"], [wn])
+                    pe(2048, [(W[w][:], T.idn[:], T.dif[:, d], False, True)], D[x] + ["idn"], [wn + "d"], [wn])
+                    act(512, T.ab[:, d], W[w][:], ACT.Abs, [wn + "d"], AB[x], [wn])
+                elif u not in FINE:
+                    name(t, "a%d" % x)
+                    act(512, T.ab[:, d], T.dif[:, d], ACT.Abs, D[x], AB[x])
+
+        def ratios(c):
+            S, sn, cols = SB[c % 2], "S%d" % (c % 2), slice(128 * c, 128 * c + 128)
+            name(t, "s%d s%d rp%d rd%d wf%d hi%d lo%d w%d h%d w%d h%d" % (2 * c, 2 * c + 1, c, c, c, c, c, 2 * c, 2 * c, 2 * c + 1, 2 * c + 1))
+            for j in range(2):
+                pe(1024, [(S[:, 16 * i:16 * i + 16], T.ab[:, 1024 * c + 128 * i:1024 * c + 128 * i + 128], T.hd2[:], True, True) for i in range(4 * j, 4 * j + 4)],
+                   AB[2 * c + j] + ["hd2a", "hd2b"], [sn + "_%d" % j], [sn])
+            act(128, T.rp[:, cols], S[:, 0:128], ACT.Relu, [sn + "_0", sn + "_1"], ["rp%d" % c], [sn], bias=0.25, scale=-1.0 / 128)
+            RB, rn = [T.R0, T.R1][c % 2], "R%d" % (c % 2)
+            pe(640, [(RB[:, 0:128], T.cb[0:1, 0:128], T.cb[0:1, 128:256], True, False), (RB[:, 0:128], T.rp[:, cols], T.dm[:], False, True)],
+               ["rp%d" % c, "cb0", "cb1", "dm"], [rn + "d"], [rn])
+            act(128, RB[:, 128:256], RB[:, 0:128], ACT.Exp, [rn + "d", "pF5"], [rn + "f"], [rn], bias=T.pF[:, 5:6])
+            act(128, T.whi[:, cols], RB[:, 0:128], ACT.Exp, [rn + "d"], ["hi%d" % c], [rn])
+            vec(128, V.tensor_tensor, (T.wlo[:, cols], RB[:, 128:256], T.whi[:, cols], ALU.subtract), [rn + "f", "hi%d" % c], ["lo%d" % c], [rn])
+            for j in range(2):
+                (w, wn), d = bank(), slice(1024 * c + 512 * j, 1024 * c + 512 * j + 512)
+                pe(512, [(W[w][:, 128 * i:128 * i + 128], T.big[:, 128 * (4 * j + i):128 * (4 * j + i) + 128], T.wlo[:, cols], True, True) for i in range(4)],
+                   BIG + ["lo%d" % c], [wn + "d"], [wn])
+                vec(512, V.tensor_tensor_scan, (T.hs[:, d], W[w][:], T.dif[:, d], 0.0, ALU.mult, ALU.add), D[2 * c + j] + [wn + "d"], ["h%d" % (2 * c + j)], [wn])
+
+        def finish(k, b, n):
+            m, c = 32 * n, (b + n - 1) // 2
+            S, sn = SB[0], "S0"
+            name(t, "ew%d u%d us%d f%d tq%d fw%d fin%d %s%d" % (k, k, k, k, k, k, k, "st" if last else "send", k))
+            act(m, T.ew[:, 32 * b:32 * b + m], T.rp[:, 64 * b:64 * (b + n):2], ACT.Exp, ["rp%d" % x for x in range(b // 2, c + 1)], ["ew%d" % k], bias=LNW)
+            pe(256 * n, [(S[0:8, 128 + 16 * i:144 + 16 * i], T.ew[:, 32 * b + 8 * i:32 * b + 8 * i + 8], T.r16[:, 16:32] if b + i // 4 in raw else T.r16[:, 0:16],
+                          True, True) for i in range(4 * n)], ["ew%d" % k] + R16, [sn + "u"], [sn])
+            act(64 * n, T.us[0:8, 64 * b:64 * (b + n)], S[0:8, 128:128 + 64 * n], ACT.Copy, [sn + "u"], [US[k]], [sn])
+            pe(256 * n, [(T.FB[:, 64 * b:64 * (b + n)], T.wide[0:33, :], T.us[0:33, 64 * b:64 * (b + n)], True, True)],
+               [US[k], "wide"], ["fs%d" % k, "fw%d" % k], ["F"])
+            tq, fw = T.tq[:, 32 * b:32 * (b + n)], T.FB[:, 64 * b + 1:64 * (b + n):2]
+            vec(m, V.tensor_tensor, (tq, T.FB[:, 64 * b:64 * (b + n):2], T.vq4[:, vo + 128 * b:vo + 128 * (b + n):4], ALU.mult),
+                ["fs%d" % k] + VR, ["tq%d" % k], ["F"])
+            vec(m, V.tensor_tensor, (fw, fw, T.hs[:, 512 * b + 15:512 * (b + n):16], ALU.mult), ["h%d" % x for x in range(b, b + n)], ["fw%d" % k], ["F"])
+            if last:
+                vec(m, V.tensor_tensor, (T.ovb[:, 64 * b:64 * (b + n):2], fw, tq, ALU.add), ["tq%d" % k, "fw%d" % k], ["ove%d" % k], ["F"])
+                dma("sp", "st%d" % k, T.yv[:, 64 * b:64 * (b + n)], T.ovb[:, 64 * b:64 * (b + n)], ["ove%d" % k, "ovo"], ())
+            else:
+                o, nm = T.vw[:, 2048 * (t + 1) + 256 * r + 32 * b:2048 * (t + 1) + 256 * r + 32 * (b + n)], "vs%d_o%d" % (t + 1, k)
+                vec(m, V.tensor_tensor, (o, fw, tq, ALU.add), ["tq%d" % k, "fw%d" % k], [nm], ["F"])
+                send(o, 4 * m, "av%d" % t, [nm], "vs%d_r" % (t + 1))
+
+        for k, (b, n) in enumerate(GROUPS):
+            for c in range(b // 2, (b + n) // 2):
+                ratios(c)
+            finish(k, b, n)
+
+    def z_layer(t):
+        if t == 0:
+            zwin, znm = T.znat[:, 0:4096], ["znat_o", "znat_r"]
+        else:
+            zwin, znm = T.zw[:, 2048 * (t - 1):2048 * (t + 1)], zslot(t - 1) + zslot(t)
+        n, s = 4096 // ZG, 4096 // ZS
+        for c in range(ZG):
+            for kb in range(4):
+                o = 256 * t + 64 * kb + n // 64 * c
+                out, src = T.zg[:, n * c + kb:n * c + n:4], zwin.indirect(T.off[:, o:o + n // 64])
+                name(t, "zg%d" % (4 * c + kb))
+                if 4 * c + kb in ZV[t]:
+                    vec(n // 4 * GATH, V.tensor_copy, (out, src), znm + ["off%d" % t], ["zg%d_%d" % (c, kb)])
+                else:
+                    act(n // 4 * GATH, out, src, ACT.Copy, znm + ["off%d" % t], ["zg%d_%d" % (c, kb)])
+        for i in range(ZS):
+            name(t, "zm%d" % i)
+            vec(s // 2, V.tensor_tensor_scan, (T.zs[:, s * i:s * i + s], T.msk[:], T.zg[:, s * i:s * i + s], 0.0, ALU.mult, ALU.max),
+                ["msk"] + ["zg%d_%d" % (i * ZG // ZS, k) for k in range(4)], ["zm%d" % i])
+        name(t, "mix bI cI")
+        pe(256, [(T.R1[:, 256:512], T.bms[:], T.zs[:, 15:4096:16], True, True)], ["bm"] + ["zm%d" % i for i in range(ZS)], ["mix"], ["R1"])
+        vec(256, V.tensor_copy, (T.bI[:], T.R1[:, 256:512]), ["mix"], ["bI"], ["R1"])
+        vec(256, V.tensor_scalar, (T.cI[:], T.bI[:], 2, 15, ALU.arith_shift_right, ALU.bitwise_and), ["bI"], ["cI"])
+        if t == R - 1:
+            a0 = 2048 * t + 256 * r
+            name(t, "ozo zo stz")
+            act(256, T.ozb[:, 1:512:2], T.zw[:, a0:a0 + 256], ACT.Copy, ["zs%d_o" % t], ["ozo"])
+            vec(256, V.tensor_copy, (T.ozb[:, 0:512:2], T.cI[:]), ["cI"], ["oze"])
+            dma("sp", "stz", T.yz[:], T.ozb[:], ["oze", "ozo"], ())
+        else:
+            a0 = 2048 * (t + 1) + 256 * r
+            name(t, "zo sendz")
+            vec(256, V.tensor_copy, (T.zw[:, a0:a0 + 256], T.cI[:]), ["cI"], ["zs%d_o" % (t + 1)])
+            send(T.zw[:, a0:a0 + 256], 512, "az%d" % t, ["zs%d_o" % (t + 1)], "zs%d_r" % (t + 1))
+
+    for t in range(R):
+        v_layer(t)
+        if t == 0:
+            odd(T.vw, T.vnat, "v")
+        if t < R - 1:
+            offsets(t + 1, 0)
+            offsets(t + 1, 1)
+        if 1 <= t < R - 1:
+            repeat(t + 1)
+        z_layer(t)
+        if t == 0:
+            odd(T.zw, T.znat, "z")
+
+    if not ORDER:
+        ORDER.extend(schedule(steps, keys(steps, group)))
     cnt = {"pe": 0, "dve": 0, "act": 0, "pool": 0, "sent": 0}
     clock = {q: {} for q in Q}
     writer, readers, touch = {}, {}, {}
+    for kind, *rest in calls:
+        if kind == "wire":
+            v = neng * (NR - 1) + (writer[rest[1]][0][1] if rest[1] in writer else 0)
+            writer[rest[1]] = [(rest[0], v, {rest[0]: v})]
 
     def sync(q, reads, writes, banks):
         need = []
         for x in reads:
-            need += writer.get(x, [])
+            need += writer[x]
         for x in writes:
             need += writer.get(x, []) + readers.get(x, [])
         for b in banks:
@@ -93,7 +521,8 @@ def rank_program(g, core, T, topo):
                 if ck.get(s, 0) < v:
                     ck[s] = v
 
-    def note(q, tok, reads, writes, banks):
+    def note(q, sem, v, reads, writes, banks):
+        tok = (sem, v, dict(clock[q], **{sem: v}))
         for x in reads:
             readers.setdefault(x, []).append(tok)
         for x in writes:
@@ -102,342 +531,27 @@ def rank_program(g, core, T, topo):
         for b in banks:
             touch.setdefault(b, {})[q] = tok
 
-    def op(q, emit, reads=(), writes=(), banks=()):
-        if q == "pool":
-            writes = list(writes) + ["poolq"]
-        sync(q, reads, writes, banks)
-        emit().then_inc(T.sem[q], 1)
-        cnt[q] += 1
-        ck = dict(clock[q])
-        ck[q] = cnt[q]
-        note(q, (q, cnt[q], ck), reads, writes, banks)
-
-    def dma(q, sem, out, in_, reads=(), writes=()):
-        sync(q, reads, writes, ())
-        Q[q].dma_start(out, in_).then_inc(T.sem[sem], 16)
-        ck = dict(clock[q])
-        ck[sem] = 16
-        note(q, (sem, 16, ck), reads, writes, ())
-
-    peers = [T.cores[(r + j) % NR] for j in range(1, NR)]
-    emask = topo.mask(core, peers[0])
-    for c in peers[1:]:
-        emask &= topo.mask(core, c)
-    neng = bin(emask).count("1")
-    ids = [DstId(rid=topo.addr(c)[0], pnc=topo.addr(c)[1]) for c in peers]
-
-    def send(ap, sem, reads):
-        sync("pool", reads, (), ())
-        g.remote_dma_fused([RemoteDMATransfer(dst_ids=ids, dma_engine_mask=emask, remote_sem=T.sem[sem], src=ap,
-                                              dsts=[ap] * len(ids))], local_sem=T.sem.sent)
-        cnt["sent"] += neng
-
-    def arrivals(name, sem, n):
-        writer[name] = [(sem, n * neng * (NR - 1), {sem: n * neng * (NR - 1)})]
-
-    arrivals("vnat_r", "vn", 1)
-    arrivals("znat_r", "zn", 1)
-    for t in range(R - 1):
-        arrivals("vs%d_r" % (t + 1), "av%d" % t, 2)
-        arrivals("zs%d_r" % (t + 1), "az%d" % t, 1)
-
-    def vec(emit, reads=(), writes=(), banks=()):
-        op("dve", emit, reads, writes, banks)
-
-    def act(emit, reads=(), writes=(), banks=()):
-        op("act", emit, reads, writes, banks)
-
-    def pe(mms, reads=(), banks=()):
-        def emit():
-            last = None
-            for m in mms:
-                last = P.matmul(*m)
-            return last
-        op("pe", emit, reads, (), banks)
-
-    def ps(name):
-        return "ps_" + name
-
-    own = 512 * r
-    dma("sp", "ldv", T.vnat[:, own:own + 512], T.v0[:], (), ["vnat_o"])
-    dma("act", "ldz", T.znat[:, own:own + 512], T.z0[:], (), ["znat_o"])
-    dma("sp", "ldy", T.axy[:, 0:128], T.ay[:], (), ["ay"])
-    dma("act", "ldx", T.axy[:, 128:256], T.ax[:], (), ["ax"])
-    dma("sp", "ldb", T.bms[:], T.bm[:], (), ["bm"])
-
-    vec(lambda: V.memset(T.posR[:], 0.0), (), ["posR"])
-    vec(lambda: V.memset(T.posL[:], 0.0), (), ["posL"])
-    op("pool", lambda: g.iota(T.pI[:, 0:1], [[0, 1]], 0, 1), (), ["p0"])
-    op("pool", lambda: g.iota(T.row[:], [[1, 128]], 0, 0, allow_small_or_imprecise_dtypes=True), (), ["row"])
-    op("pool", lambda: g.iota(T.permf[:], [[128, 2], [2, 8]], 0, 0, allow_small_or_imprecise_dtypes=True), (), ["permf"])
-    op("pool", lambda: g.iota(T.posR[32:33, :], [[256, 16], [0, 2], [16, 16]], 0, 0, allow_small_or_imprecise_dtypes=True),
-       ["posR"], ["posRx"])
-    vec(lambda: V.memset(T.msk[:], 1.0), (), ["msk"])
-    for q4 in range(4):
-        vec(lambda q4=q4: V.memset(T.posR[0:1, 128 * q4:128 * q4 + 128], float(64 * (4 * r + q4))), ["posR"], ["posRy%d" % q4])
-    vec(lambda: V.memset(T.posR[64:65, :], 1.0), ["posR"], ["posR1"])
-    vec(lambda: V.memset(T.posL[0:1, 0:128:2], 1.0), ["posL"], ["posL0"])
-    vec(lambda: V.memset(T.posL[32:33, 1:128:2], 1.0), ["posL"], ["posL1"])
-    vec(lambda: V.memset(T.posL[64:65, 1:128:2], 8.0), ["posL"], ["posL2"])
-    vec(lambda: V.memset(T.msk[:, 0:2048:16], 0.0), (), ["msk"])
-    POS = ["posRx", "posR1", "posL0", "posL1", "posL2"] + ["posRy%d" % i for i in range(4)]
-    vec(lambda: V.tensor_scalar(T.pI[:, 1:2], T.pI[:, 0:1], 7, None, ALU.bitwise_and), ["p0"], ["p1"])
-    vec(lambda: V.tensor_scalar(T.pI[:, 2:3], T.pI[:, 0:1], 4, None, ALU.arith_shift_right), ["p0"], ["p2"])
-    vec(lambda: V.tensor_scalar(T.pI[:, 3:4], T.pI[:, 0:1], 3, 1, ALU.arith_shift_right, ALU.bitwise_and), ["p0"], ["p3"])
-    vec(lambda: V.tensor_copy(T.pF[:, 0:4], T.pI[:, 0:4]), ["p0", "p1", "p2", "p3"], ["pF"])
-    act(lambda: A.activation(T.c32[:], T.row[:], ACT.Exp, bias=-math.log(32.0), scale=0.0), ["row"], ["c32"])
-    vec(lambda: V.tensor_scalar(T.idn[:], T.row[:], T.pF[:, 0:1], None, ALU.is_equal), ["row", "pF"], ["idn"])
-    vec(lambda: V.tensor_scalar(T.pF[:, 4:5], T.pF[:, 1:2], 16.0, T.pF[:, 3:4], ALU.mult, ALU.add), ["pF"], ["pF4"])
-    vec(lambda: V.tensor_scalar(T.hd[:], T.row[:, 0:8], T.pF[:, 2:3], None, ALU.is_equal), ["row", "pF"], ["hd"])
-    vec(lambda: V.tensor_scalar(T.prm[:], T.permf[:], T.pF[:, 4:5], None, ALU.add), ["permf", "pF4"], ["perm"])
-
-    send(T.vnat[:, own:own + 512], "vn", ["vnat_o"])
-    send(T.znat[:, own:own + 512], "zn", ["znat_o"])
-    op("pool", lambda: g.iota(T.row2[:], [[1, 8], [0, 16]], 0, 0, allow_small_or_imprecise_dtypes=True), (), ["row2"])
-
-    LHS = []
-    for gp in range(2):
-        for a in range(4):
-            o, i = 128 * gp + 32 * a, 32 * a + 16 * gp
-            vec(lambda o=o, i=i: V.tensor_scalar(T.lhs[:, o:o + 32:2], T.axy[:, i:i + 16], 8.0, None, ALU.mult), ["ay"], ["ly%d" % o])
-            act(lambda o=o, i=i: A.activation(T.lhs[:, o + 1:o + 32:2], T.axy[:, 128 + i:128 + i + 16], ACT.Copy), ["ax"], ["lx%d" % o])
-            LHS += ["ly%d" % o, "lx%d" % o]
-
-    def idx_mm(t):
-        kk = 64 if t % 2 == 0 else 96
-        mms = [(T.EB[:, 0:512], T.posL[0:kk, :], T.posR[0:kk, :], True, False)]
-        for blk in range(16):
-            if t < 2:
-                a0 = own + 32 * blk + t
-                zq = T.znat[:, a0:a0 + 31:2]
-            else:
-                a0 = 2048 * (t - 1) + 256 * r + 16 * blk
-                zq = T.zw[:, a0:a0 + 16]
-            for gp in range(2):
-                c0 = 32 * blk + 16 * gp
-                mms.append((T.EB[:, c0:c0 + 16], T.lhs[:, 128 * gp:128 * gp + 128], zq, False, blk == 15 and gp == 1))
-        src = "znat_o" if t < 2 else "zs%d_o" % (t - 1)
-        sync("pe", (), ["EB"], ())
-        pe(mms, POS + LHS + [src], [ps("E")])
-        writer["EB"] = [touch[ps("E")]["pe"]]
-        readers["EB"] = []
-
-    def idx_ops(t):
-        o = T.off[:, 256 * t:256 * t + 256]
-        ops = [lambda: vec(lambda: V.transpose(T.eT[:], T.EB[:]), ["EB"], ["eT"], [ps("E")]),
-               lambda: vec(lambda: V.tensor_copy(T.eI[:], T.eT[:]), ["eT"], ["eI"]),
-               lambda: vec(lambda: V.tensor_scalar(T.yI[:], T.eI[:, 0:512:2], 0x7C0, None, ALU.bitwise_and), ["eI"], ["yI"])]
-        if t == 0:
-            ops += [lambda: vec(lambda: V.tensor_scalar(T.uI[:], T.eI[:, 1:512:2], 3, 127, ALU.arith_shift_right, ALU.bitwise_and), ["eI"], ["uI"]),
-                    lambda: vec(lambda: V.tensor_scalar(T.EB[:, 0:256], T.yI[:], 2.0, None, ALU.mult), ["yI"], ["EB"], [ps("E")]),
-                    lambda: vec(lambda: V.tensor_tensor(T.tI[:], T.EB[:, 0:256], T.uI[:], ALU.add), ["EB", "uI"], ["tI"], [ps("E")])]
-        else:
-            ops += [lambda: vec(lambda: V.tensor_scalar(T.uI[:], T.eI[:, 1:512:2], 0x3F8, None, ALU.bitwise_and), ["eI"], ["uI"]),
-                    lambda: vec(lambda: V.tensor_scalar(T.EB[:, 0:256], T.uI[:], 256.0625, 2048.0 * (t % 2) - 0.25, ALU.mult, ALU.add),
-                                ["uI"], ["EB"], [ps("E")]),
-                    lambda: vec(lambda: V.tensor_tensor(T.sI[:], T.EB[:, 0:256], T.yI[:], ALU.add), ["EB", "yI"], ["sI"], [ps("E")]),
-                    lambda: vec(lambda: V.tensor_scalar(T.tI[:], T.sI[:], 0xFFF, None, ALU.bitwise_and), ["sI"], ["tI"])]
-        ops.append(lambda: vec(lambda: V.tensor_copy(o, T.tI[:, 0:256].indirect(T.prm[:, 0:16])), ["tI", "perm"], ["off%d" % t]))
-        return ops
-
-    def vrep(t):
-        for c in range(2):
-            if t < 2:
-                a0 = own + 256 * c + t
-                src, nm = T.vnat[:, a0:a0 + 255:2], "vnat_o"
-            else:
-                a0 = 2048 * (t - 1) + 256 * r + 128 * c
-                src, nm = T.vw[:, a0:a0 + 128], "vs%d_o%d" % (t - 1, c)
-            for j in range(4):
-                o = 1024 * (t % 2) + 512 * c + 128 * j
-                act(lambda o=o, src=src: A.activation(T.vrep[:, o:o + 128], src, ACT.Copy), [nm], ["vr%d" % o])
-
-    idx_mm(0)
-    for f in idx_ops(0):
-        f()
-    vrep(0)
-    vec(lambda: V.tensor_scalar(T.sal[:], T.row2[:], T.pF[:, 1:2], None, ALU.is_equal), ["row2", "pF"], ["sal"])
-    BIG = []
-    for c in range(16):
-        act(lambda c=c: A.activation(T.big[:, c:2048:16], T.idn[:], ACT.Copy), ["idn"], ["big%d" % c])
-        BIG.append("big%d" % c)
-    op("pool", lambda: g.affine_select(T.zw[:, 0:2048], T.znat[:, 1:4096:2], [[0, 2048]], ALU.is_ge, 0.0, 0, 0),
-       ["znat_o", "znat_r"], ["zs0_o"])
-
-    W = [T.W0, T.W1, T.W2, T.W3]
-    SB, SN = [T.ST, T.W3], [ps("S"), ps("W3")]
-    LNW = -0.25 - math.log(64.0)
-
-    for t in range(R):
-        last = t == R - 1
-        if t == 0:
-            vwin, vnm = T.vnat[:, 0:4096], ["vnat_o", "vnat_r"]
-            zwin, znm = T.znat[:, 0:4096], ["znat_o", "znat_r"]
-        else:
-            vwin, zwin = T.vw[:, 2048 * (t - 1):2048 * (t + 1)], T.zw[:, 2048 * (t - 1):2048 * (t + 1)]
-            vnm = ["vs%d_%s" % (s, x) for s in (t - 1, t) for x in ("o0", "o1", "r")]
-            znm = ["zs%d_%s" % (s, x) for s in (t - 1, t) for x in ("o", "r")]
-        offn = "off%d" % t
-        ob = 256 * t
-        bank = [[0, 1, 2, 3], [1, 2, 3, 0]]
-
-        def dcol(c, b):
-            return 2048 * c + 512 * b
-
-        def gat(c, b):
-            d, vo = dcol(c, b), 1024 * (t % 2) + 512 * c
-            o = ob + 128 * c + 32 * b
-            vec(lambda: V.tensor_tensor(T.dif[:, d:d + 512], vwin.indirect(T.off[:, o:o + 32]), T.vrep[:, vo:vo + 512], ALU.subtract),
-                vnm + [offn] + ["vr%d" % (vo + 128 * j) for j in range(4)], ["d%d" % d])
-
-        def absb(c, b):
-            d = dcol(c, b)
-            act(lambda: A.activation(T.ab[:, d:d + 512], T.dif[:, d:d + 512], ACT.Abs), ["d%d" % d], ["a%d" % d])
-
-        def smm(c, b):
-            d = dcol(c, b)
-            pe([(SB[c][:, 8 * (4 * b + j):8 * (4 * b + j) + 8], T.ab[:, d + 128 * j:d + 128 * j + 128], T.hd[:], True, True)
-                for j in range(4)], ["a%d" % d, "hd"], [SN[c]])
-
-        def relu(c):
-            act(lambda: A.activation(T.rT[:, 128 * c:128 * c + 128], SB[c][:, 0:128], ACT.Relu, bias=0.25, scale=-1.0 / 128),
-                (), ["rT%d" % c], [SN[c]])
-
-        def turn(c):
-            op("pe", lambda: P.transpose(T.RB[:, 0:128], T.rT[:, 128 * c:128 * c + 128], T.idn[:]), ["rT%d" % c, "idn"], (), [ps("R")])
-
-        def expo(c):
-            act(lambda: A.activation(T.RB[:, 128:256], T.RB[:, 0:128], ACT.Exp, bias=LNW, scale=1.0), (), ["wf"], [ps("R")])
-            act(lambda: A.activation(T.whi[:, 128 * c:128 * c + 128], T.RB[:, 0:128], ACT.Exp, bias=LNW, scale=1.0), (), ["hi%d" % c], [ps("R")])
-
-        def low(c):
-            vec(lambda: V.tensor_tensor(T.wlo[:, 128 * c:128 * c + 128], T.RB[:, 128:256], T.whi[:, 128 * c:128 * c + 128], ALU.subtract),
-                ["wf", "hi%d" % c], ["lo%d" % c], [ps("R")])
-
-        def spread(c, b):
-            w = bank[c][b]
-            mms = []
-            for j in range(4):
-                k = 4 * b + j
-                mms.append((W[w][:, 128 * j:128 * j + 128], T.big[:, 128 * k:128 * k + 128], T.whi[:, 128 * c:128 * c + 128], True, False))
-                mms.append((W[w][:, 128 * j:128 * j + 128], T.big[:, 128 * k:128 * k + 128], T.wlo[:, 128 * c:128 * c + 128], False, True))
-            pe(mms, BIG + ["hi%d" % c, "lo%d" % c], [ps("W%d" % w)])
-
-        def sumw(c):
-            o = T.FB[:, 256 + 128 * c:384 + 128 * c]
-            pe([(o, T.sal[:], T.whi[:, 128 * c:128 * c + 128], True, False), (o, T.sal[:], T.wlo[:, 128 * c:128 * c + 128], False, False),
-                (o, T.sal[:], T.c32[:], False, True)], ["sal", "c32", "hi%d" % c, "lo%d" % c], [ps("F")])
-
-        def tterm(c):
-            vo = 1024 * (t % 2) + 512 * c
-            vec(lambda: V.tensor_tensor(T.tq[:, 128 * c:128 * c + 128], T.FB[:, 256 + 128 * c:384 + 128 * c], T.vrep[:, vo:vo + 128], ALU.mult),
-                ["vr%d" % vo], ["tq%d" % c], [ps("F")])
-
-        def mul(c, b, keep):
-            d, w = dcol(c, b), bank[c][b]
-            if keep:
-                vec(lambda: V.tensor_tensor(W[w][:], W[w][:], T.dif[:, d:d + 512], ALU.mult), ["d%d" % d], ["Wv%d" % w], [ps("W%d" % w)])
-            else:
-                vec(lambda: V.tensor_tensor(T.dif[:, d:d + 512], W[w][:], T.dif[:, d:d + 512], ALU.mult), (), ["d%d" % d], [ps("W%d" % w)])
-
-        def add(c, bw, b, keep):
-            d, w = dcol(c, b), bank[c][bw]
-            if keep:
-                vec(lambda: V.tensor_tensor(W[w][:], W[w][:], T.dif[:, d:d + 512], ALU.add), ["d%d" % d], ["Wv%d" % w], [ps("W%d" % w)])
-            else:
-                vec(lambda: V.tensor_tensor(T.dif[:, d:d + 512], W[w][:], T.dif[:, d:d + 512], ALU.add), ["Wv%d" % w], ["d%d" % d], [ps("W%d" % w)])
-
-        def fold(c, b, first, end):
-            d = dcol(c, b)
-            pe([(T.FB[:, 128 * c:128 * c + 128], T.idn[:], T.dif[:, d + 128 * j:d + 128 * j + 128], first and j == 0, end and j == 3)
-                for j in range(4)], ["d%d" % d, "idn"], [ps("F")])
-
-        def fin(c):
-            if last:
-                o, nm = T.ovb[:, 256 * c:256 * c + 256:2], "ove%d" % c
-            else:
-                a0 = 2048 * (t + 1) + 256 * r + 128 * c
-                o, nm = T.vw[:, a0:a0 + 128], "vs%d_o%d" % (t + 1, c)
-            vec(lambda: V.tensor_tensor(o, T.FB[:, 128 * c:128 * c + 128], T.tq[:, 128 * c:128 * c + 128], ALU.add),
-                ["tq%d" % c], [nm], [ps("F")])
-            if last:
-                dma("sp", "st%d" % c, T.yv[:, 256 * c:256 * c + 256], T.ovb[:, 256 * c:256 * c + 256], [nm, "ovo"], ())
-            else:
-                send(o, "av%d" % t, [nm])
-
-        zn = [0]
-
-        def zgat(n):
-            for _ in range(n):
-                c, k = divmod(zn[0], 16)
-                zn[0] += 1
-                o = ob + 128 * c + 8 * k
-                act(lambda: A.activation(T.zg[:, 2048 * c + k:2048 * c + 2048:16], zwin.indirect(T.off[:, o:o + 8]), ACT.Copy),
-                    znm + [offn], ["zg%d_%d" % (c, k)])
-
-        def scan(c):
-            vec(lambda: V.tensor_tensor_scan(T.zs[:, 2048 * c:2048 * c + 2048], T.msk[:], T.zg[:, 2048 * c:2048 * c + 2048], 0.0, ALU.mult, ALU.max),
-                ["msk"] + ["zg%d_%d" % (c, k) for k in range(16)], ["zm%d" % c])
-
-        def mix():
-            pe([(T.ST[:, 256:512], T.bms[:], T.zs[:, 15:4096:16], True, True)], ["bm", "zm0", "zm1"], [ps("S")])
-
-        def zu1():
-            vec(lambda: V.tensor_copy(T.bI[:], T.ST[:, 256:512]), (), ["bI"], [ps("S")])
-
-        def zu2():
-            vec(lambda: V.tensor_scalar(T.cI[:], T.bI[:], 2, 15, ALU.arith_shift_right, ALU.bitwise_and), ["bI"], ["cI"])
-
-        def zu3():
-            if last:
-                vec(lambda: V.tensor_copy(T.ozb[:, 0:512:2], T.cI[:]), ["cI"], ["oze"])
-                dma("act", "st2", T.yz[:], T.ozb[:], ["oze", "ozo"], ())
-            else:
-                a0 = 2048 * (t + 1) + 256 * r
-                vec(lambda: V.tensor_copy(T.zw[:, a0:a0 + 256], T.cI[:]), ["cI"], ["zs%d_o" % (t + 1)])
-                send(T.zw[:, a0:a0 + 256], "az%d" % t, ["zs%d_o" % (t + 1)])
-
-        ix = []
-        if not last:
-            idx_mm(t + 1)
-            ix = idx_ops(t + 1)
-
-        def nxt(n):
-            for _ in range(n):
-                if ix:
-                    ix.pop(0)()
-
-        for b in range(4):
-            gat(0, b); absb(0, b); smm(0, b)
-        gat(1, 0); absb(1, 0); relu(0); turn(0); smm(1, 0)
-        gat(1, 1); absb(1, 1); smm(1, 1); expo(0)
-        gat(1, 2); low(0); spread(0, 0); absb(1, 2); smm(1, 2)
-        gat(1, 3); spread(0, 1); sumw(0); absb(1, 3); zgat(2); smm(1, 3)
-        mul(0, 0, True); mul(0, 1, False); tterm(0)
-        spread(0, 2); relu(1); turn(1); spread(0, 3); zgat(1); expo(1)
-        add(0, 0, 1, True); mul(0, 2, False); low(1)
-        zgat(29)
-        sumw(1); spread(1, 0); spread(1, 1)
-        add(0, 0, 2, True); mul(0, 3, False); spread(1, 2); tterm(1); add(0, 0, 3, False)
-        fold(0, 3, True, True); spread(1, 3)
-        mul(1, 0, True); mul(1, 1, False); fin(0); add(1, 0, 1, False)
-        fold(1, 1, True, False)
-        mul(1, 2, True); mul(1, 3, False); add(1, 2, 3, False)
-        fold(1, 3, False, True)
-        if last:
-            scan(0); fin(1); scan(1); mix(); zu1(); zu2(); zu3()
-        else:
-            nxt(2); fin(1)
-            if t == 0:
-                act(lambda: A.activation(T.vw[:, 0:2048], T.vnat[:, 1:4096:2], ACT.Copy), ["vnat_o", "vnat_r"], ["vs0_o0"])
-            vrep(t + 1)
-            scan(0); nxt(2); scan(1); mix(); nxt(2); zu1(); nxt(1); zu2(); nxt(1); zu3()
-            if t == R - 2:
-                a0 = 2048 * (t + 1) + 256 * r
-                act(lambda: A.activation(T.ovb[:, 1:512:2], T.vw[:, a0:a0 + 256], ACT.Copy), ["vs%d_o0" % (t + 1), "vs%d_o1" % (t + 1)], ["ovo"])
-                act(lambda: A.activation(T.ozb[:, 1:512:2], T.zw[:, a0:a0 + 256], ACT.Copy), ["zs%d_o" % (t + 1)], ["ozo"])
+    for i in ORDER:
+        q, _, _, reads, writes, banks = steps[i]
+        kind, *rest = calls[i]
+        if kind == "op":
+            if q == "pool":
+                writes = writes + ["poolq"]
+            sync(q, reads, writes, banks)
+            rest[0](*rest[1], **rest[2]).then_inc(T.sem[q], 1)
+            cnt[q] += 1
+            note(q, q, cnt[q], reads, writes, banks)
+        elif kind == "dma":
+            sync(q, reads, writes, ())
+            Q[q].dma_start(rest[1], rest[2]).then_inc(T.sem[rest[0]], 16)
+            note(q, rest[0], 16, reads, writes, ())
+        elif kind == "send":
+            sync(q, reads, (), ())
+            g.remote_dma_fused([RemoteDMATransfer(dst_ids=ids, dma_engine_mask=emask, remote_sem=T.sem[rest[1]], src=rest[0],
+                                                  dsts=[rest[0]] * len(ids))], local_sem=T.sem.sent)
+            cnt["sent"] += neng
 
     for s in ("pe", "dve", "act", "pool", "sent"):
         g.wait_ge(T.sem[s], cnt[s])
-    for s in ("st0", "st1", "st2"):
+    for s in ["stz"] + ["st%d" % c for c in range(NG)]:
         g.wait_ge(T.sem[s], 16)

import math
from concourse.bass import DstId, RemoteDMATransfer
from concourse.mybir import AluOpType as ALU, ActivationFunctionType as ACT

R = 5
NR = 8
UNITS = [(0, 2), (2, 2), (4, 2), (6, 2)]
GROUPS = [(0, 4), (4, 4)]
RAW = [[], [], [], [], []]
FINE = [0, 1, 2, 3]
ZG, ZS = 2, 4
ZV = [[6, 7], [6, 7], [6, 7], [6, 7], [7]]
NG = len(GROUPS)
NW = 2
CYC, PEC, GATH = 0.9, 0.46, 1.56
FIX = {"dve": 55.0, "act": 70.0, "pe": 0.0, "pool": 170.0}
HOP, LOAD, ISSUE, FIRST, LAND = 100.0, 2400.0, 400.0, 2000.0, 1600.0
ROW, RATE = 25.0, 20.0
QUEUES = {
    "dve": "g00 g01 g02 g03 g11 g10 g12 g13 g20 g21 g22 g23 lo0 g31 g32 g30 h0 lo1 h1 g33 h2 h3 tq0 fw0 lo2 fin0 h4 lo3 h5 h6 h7 tq1 fw1 fin1 "
           "zg7 zg6 zm1 zm2 zm0 zm3 off+ bI cI zo",
    "act": "a00 a01 a02 a03 kilo+ a11 a10 a12 rp0 a13 a20 hi0 wf0 a21 a22 rp1 a23 ew0 hi1 wf1 a30 a32 a31 rp2 us0 a33 hi2 wf2 zg1 rp3 ew1 hi3 wf3 "
           "zg0 us1 zg2 zg3 zg4 zg5 fh+ fy+ fx+",
    "pe": "mm+ s1 s0 rd0 s2 s3 w1 w0 rd1 s4 u0 s5 w2 w3 rd2 f0 s7 s6 w4 rd3 w5 u1 w6 w7 f1 mod+ sum+ mix",
    "pool": "ov0 ov1 ov2 ov3 vr0+ vr1+ vr2+ vr3+ send0 send1 oz0 oz1 oz2 sendz oz3",
}
LAST = {
    "dve": "g02 g00 g01 g03 g10 g12 g11 g13 g21 g20 g22 g31 g23 g32 g33 g30 lo0 zg7 h1 lo1 h0 h3 lo2 h2 h5 h4 fw0 tq0 lo3 zm0 zm1 h7 h6 zm3 zm2 "
           "tq1 fw1 bI fin0 cI fin1 zo",
    "act": "ovo a02 a00 a01 a03 a10 ozo a12 a11 rp0 a13 a21 a20 wf0 a22 a31 rp1 a23 hi0 a32 a33 wf1 a30 ew0 hi1 rp2 zg1 zg2 hi2 wf2 rp3 zg3 us0 wf3 hi3 "
           "zg0 zg6 zg4 ew1 zg5 us1",
    "pe": "s1 s0 rd0 s2 s3 rd1 s5 s4 w1 w0 s6 rd2 u0 w3 s7 w2 w5 rd3 w4 f0 w6 w7 u1 f1 mix",
    "sp": "st0 st1 stz",
}


def keys(steps, group):
    key, out = {}, []
    for t in range(R):
        for q, names in (LAST if t == R - 1 else QUEUES).items():
            for i, x in enumerate(names.split()):
                key[q, x.strip("+-"), t + x.count("+") - x.count("-")] = 1000 * t + i
    for i, (x, t) in enumerate(group):
        out.append(out[-1] if steps[i][0] == "wire" else i - 10000 if x is None else key[steps[i][0], x, t])
    return out


SCRATCH = {
    "vnat": ("sbuf", [128, 4096], "bfloat16"),
    "znat": ("sbuf", [128, 4096], "bfloat16"),
    "vw": ("sbuf", [128, 5 * 2048], "float32"),
    "zw": ("sbuf", [128, 5 * 2048], "bfloat16"),
    "dif": ("sbuf", [128, 4096], "float32"),
    "ab": ("sbuf", [128, 4096], "float32"),
    "hs": ("sbuf", [128, 4096], "float32"),
    "zg": ("sbuf", [128, 4096], "bfloat16"),
    "zs": ("sbuf", [128, 4096], "bfloat16"),
    "msk": ("sbuf", [128, 4096 // ZS], "bfloat16"),
    "vq4": ("sbuf", [128, 2048], "float32"),
    "off": ("sbuf", [128, 5 * 256], "uint16"),
    "fld": ("sbuf", [128, 1280], "bfloat16"),
    "dg": ("sbuf", [128, 512], "bfloat16"),
    "bI": ("sbuf", [128, 256], "int32"),
    "cI": ("sbuf", [128, 256], "int32"),
    "pI": ("sbuf", [128, 8], "int32"),
    "pF": ("sbuf", [128, 8], "float32"),
    "row": ("sbuf", [128, 128], "float32"),
    "idn": ("sbuf", [128, 128], "float32"),
    "nid": ("sbuf", [128, 128], "float32"),
    "dm": ("sbuf", [128, 128], "float32"),
    "j2": ("sbuf", [128, 64], "float32"),
    "r16": ("sbuf", [128, 32], "float32"),
    "hd2": ("sbuf", [128, 16], "float32"),
    "wide": ("sbuf", [128, 128], "float32"),
    "big": ("sbuf", [128, 1024], "bfloat16"),
    "cb": ("sbuf", [128, 256], "bfloat16"),
    "posL": ("sbuf", [128, 128], "bfloat16"),
    "posR": ("sbuf", [128, 512], "bfloat16"),
    "axy": ("sbuf", [128, 256], "bfloat16"),
    "bms": ("sbuf", [128, 128], "bfloat16"),
    "mk": ("sbuf", [128, 288], "bfloat16"),
    "lhs": ("sbuf", [128, 16 + 8 * 144], "bfloat16"),
    "rp": ("sbuf", [128, 512], "float32"),
    "ew": ("sbuf", [128, 256], "float32"),
    "us": ("sbuf", [128, 512], "float32"),
    "whi": ("sbuf", [128, 512], "bfloat16"),
    "wlo": ("sbuf", [128, 512], "float16"),
    "tq": ("sbuf", [128, 256], "float32"),
    "ovb": ("sbuf", [128, 512], "float32"),
    "ozb": ("sbuf", [128, 512], "float32"),
    "W0": ("psum", [128, 512], "float32"),
    "W1": ("psum", [128, 512], "float32"),
    "S0": ("psum", [128, 512], "float32"),
    "S1": ("psum", [128, 512], "float32"),
    "R0": ("psum", [128, 512], "float32"),
    "R1": ("psum", [128, 512], "float32"),
    "FB": ("psum", [128, 512], "float32"),
    "EB": ("psum", [128, 512], "float32"),
}
SEMAPHORES = (["pe", "dve", "act", "pool", "sent", "ldv", "ldz", "ldy", "ldx", "ldb", "stz", "vn", "zn"]
              + ["st%d" % i for i in range(NG)] + ["av%d" % i for i in range(4)] + ["az%d" % i for i in range(4)])
ORDER = []


def schedule(steps, key):
    n = len(steps)
    preds, writer, readers = [], {}, {}
    for i, (q, d, lag, reads, writes, banks) in enumerate(steps):
        p = set()
        for x in reads:
            p.update(writer[x])
        for x in writes:
            if not x.endswith("_r"):
                p.update(writer.get(x, []) + readers.get(x, []))
        preds.append(p)
        for x in reads:
            readers.setdefault(x, []).append(i)
        for x in writes:
            writer[x] = (writer.get(x, []) if x.endswith("_r") else []) + [i]
            readers[x] = []
    queues = {}
    for i in sorted(range(n), key=lambda k: (key[k], k)):
        queues.setdefault(steps[i][0], []).append(i)
    free, done, bank, order = {q: 0.0 for q in queues}, {}, {}, []
    while len(order) < n:
        heads = [l[0] for l in queues.values() if l and all(p in done for p in preds[l[0]])]
        t, i = min((max([free[steps[k][0]]] + [done[p] for p in preds[k]]
                        + [e for b in steps[k][5] for o, e in bank.get(b, {}).items() if o != steps[k][0]]), k) for k in heads)
        q, d, lag = steps[i][:3]
        order.append(queues[q].pop(0))
        free[q], done[i] = t + d, t + d + lag
        for b in steps[i][5]:
            bank.setdefault(b, {})[q] = t + d + HOP
    return order


def rank_program(g, core, T, topo):
    r = T.rank_of(core)
    if r is None:
        return
    Q = {"pe": g.tensor, "dve": g.vector, "act": g.scalar, "pool": g, "sp": g.sync}
    V, A, P = g.vector, g.scalar, g.tensor
    steps, calls, group, names = [], [], [], []

    peers = [T.cores[(r + j) % NR] for j in range(1, NR)]
    emask = topo.mask(core, peers[0])
    for c in peers[1:]:
        emask &= topo.mask(core, c)
    neng = bin(emask).count("1")
    ids = [DstId(rid=topo.addr(c)[0], pnc=topo.addr(c)[1]) for c in peers]

    def step(s, call):
        steps.append(s)
        calls.append(call)
        group.append(names.pop(0) if names and s[0] != "wire" else (None, 0))

    def name(t, text):
        names.extend((x, t) for x in text.split())

    def op(q, cycles, fn, args, reads, writes, banks, kw=None):
        step((q, FIX[q] + max(cycles, 64) * (PEC if q == "pe" else CYC), HOP, list(reads), list(writes), list(banks)), ("op", fn, args, kw or {}))

    def vec(cycles, fn, args, reads=(), writes=(), banks=()):
        op("dve", cycles, fn, args, reads, writes, banks)

    def act(cycles, out, in_, func, reads=(), writes=(), banks=(), **kw):
        op("act", cycles, A.activation, (out, in_, func), reads, writes, banks, kw)

    def pool(n, fn, args, reads=(), writes=(), **kw):
        op("pool", 2 * n, fn, args, reads, writes, (), kw)

    def matmuls(mms):
        return [P.matmul(*m) for m in mms][-1]

    def pe(cycles, mms, reads=(), writes=(), banks=()):
        op("pe", cycles, matmuls, (mms,), reads, writes, banks)

    def dma(q, sem, out, in_, reads=(), writes=()):
        step((q, 60.0, LOAD, list(reads), list(writes), []), ("dma", sem, out, in_))

    nsent = [0]

    def send(ap, nbytes, sem, reads, arrival):
        nsent[0] += 1
        step(("pool", ISSUE, FIRST if nsent[0] == 1 else 0.0, list(reads), ["issue%d" % nsent[0]], []), ("send", ap, sem))
        step(("wire", 128 * (NR - 1) / neng * (ROW + nbytes / RATE), LAND, ["issue%d" % nsent[0]], [arrival], []), ("wire", sem, arrival))

    def iota(n, out, pattern, base, cm, reads, writes):
        pool(n, g.iota, (out, pattern, base, cm), reads, writes, allow_small_or_imprecise_dtypes=True)

    def fill(n, ap, value, reads, writes):
        vec(n, V.memset, (ap, value), reads, writes)

    def equal(n, out, in_, col, writes):
        vec(n, V.tensor_scalar, (out, in_, T.pF[:, col:col + 1], None, ALU.is_equal), ["row", "pF", "pF2"], writes)

    def const(n, out, like, value, writes):
        act(n, out, like, ACT.Identity, ["znat_o"], writes, scale=0.0, bias=value)

    def vslot(s):
        return ["vs0_%d" % i for i in range(4)] if s == 0 else ["vs%d_r" % s] + ["vs%d_o%d" % (s, c) for c in range(NG)]

    def zslot(s):
        return ["zs0_%d" % i for i in range(4)] if s == 0 else ["zs%d_r" % s, "zs%d_o" % s]

    own = 512 * r
    POS = ["posRy", "posRx", "posR1", "posR2", "posL0", "posL1", "posL2"]
    LHS = ["lhs%d" % i for i in range(8)]
    MK = ["mk%d" % i for i in range(8)]
    BIG = ["big%d" % c for c in range(16)]
    US = ["us%d" % c for c in range(NG)]
    DG = ["dg%d" % i for i in range(4)]
    BASE = 1.5 * 2 ** 17

    def offsets(t, part):
        E, en, ed = T.EB, "E", ["EB"]
        kk = 64 if t % 2 == 0 else 96
        mms = [(E[:, 0:512], T.posL[0:kk, :], T.posR[0:kk, :], True, False)]
        for i in range(8):
            for ql in range(4):
                if t < 2:
                    zq = T.znat[:, own + 2 * ql + t:own + 512:8]
                else:
                    a0 = 2048 * (t - 1) + 256 * r
                    zq = T.zw[:, a0 + ql:a0 + 256:4]
                o = 16 + 144 * i + 4 * (i % 4 - ql)
                mms.append((E[:, 64 * i:64 * i + 64], T.lhs[:, o:o + 128], zq, False, False))
        src = POS + LHS + ["znat_o" if t < 2 else "zs%d_o" % (t - 1)]
        if part == 0:
            if t > 0:
                name(t, "mm")
            return pe(2560, mms[:-1] + [mms[-1][:4] + (True,)], src, ed, [en])
        if t > 0:
            name(t, "kilo mod fy fx fh sum off")

        def floor(out, src, unit, scale, nm):
            act(256, out, src, ACT.Identity, ed, [nm], [en], scale=scale, bias=scale * (BASE + 129 * unit - unit / 2 + 0.5))
            return scale * 129 * unit

        one, minus, up, down = [T.dg[:, 128 * i:128 * i + 128] for i in range(4)]
        fy, fx, fh = T.fld[:, 512:768], T.fld[:, 768:1024], T.fld[:, 1024:1280]
        act(512, T.fld[:, 0:512], E[:], ACT.Identity, ed, ["kilo"], [en], bias=BASE - 511.5)
        pe(3072, mms + [(E[:], minus, T.fld[:, 0:512], False, True)], ["kilo", "dg1"] + src, ed, [en])
        if t == 0:
            c = floor(fy, E[:, 0:256], 32, 4.0, "fy") + floor(fx, E[:, 256:512], 8, 0.125, "fx")
            terms, nm = [(one, fy), (one, fx)], ["fy", "fx"]
        else:
            cy, cx, ch = floor(fy, E[:, 0:256], 32, 2.0, "fy"), floor(fx, E[:, 256:512], 8, 256.0, "fx"), floor(fh, E[:, 256:512], 16, 0.0625, "fh")
            sg = 1 - 2 * (t % 2)
            c = cy + ch + sg * (cx - 4096 * ch) - 2048 * (t % 2)
            terms, nm = [(one, fy), (one, fh), (minus if t % 2 else one, fx), (up if t % 2 else down, fh)], ["fy", "fx", "fh"]
        pe(256 * len(terms), [(E[:, 0:256], a, b, i == 0, i == len(terms) - 1) for i, (a, b) in enumerate(terms)], nm + DG, ed, [en])
        vec(256, V.tensor_scalar, (T.off[:, 256 * t:256 * t + 256], E[:, 0:256], -c, None, ALU.add), ed, ["off%d" % t], [en])

    def repeat(t):
        if t < 2:
            src, nm = T.vnat[:, own + t:own + 512:2], ["vnat_o"]
        else:
            a0 = 2048 * (t - 1) + 256 * r
            src, nm = T.vw[:, a0:a0 + 256], vslot(t - 1)[1:]
            name(t, "vr0 vr1 vr2 vr3")
        for j in range(4):
            o = T.vq4[:, 1024 * (t % 2) + j:1024 * (t % 2) + 1024:4]
            if t < 2:
                act(256, o, src, ACT.Copy, nm, ["vr%d_%d" % (t % 2, j)])
            else:
                pool(256, g.affine_select, (o, src, [[0, 256]], ALU.is_ge, 0.0, 0, 0), nm, ["vr%d_%d" % (t % 2, j)])

    def odd(dst, src, nm):
        for i in range(4):
            name(0, "o%s%d" % (nm, i))
            pool(512, g.affine_select, (dst[:, 512 * i:512 * i + 512], src[:, 1024 * i + 1:1024 * i + 1024:2], [[0, 512]], ALU.is_ge, 0.0, 0, 0),
                 [nm + "nat_o", nm + "nat_r"], [nm + "s0_%d" % i])

    dma("sp", "ldv", T.vnat[:, own:own + 512], T.v0[:], (), ["vnat_o"])
    dma("act", "ldz", T.znat[:, own:own + 512], T.z0[:], (), ["znat_o"])
    dma("sp", "ldy", T.axy[:, 0:128], T.ay[:], (), ["ay"])
    dma("act", "ldx", T.axy[:, 128:256], T.ax[:], (), ["ax"])
    dma("sp", "ldb", T.bms[:], T.bm[:], (), ["bm"])
    fill(256, T.posR[:], 0.0, (), ["posR"])
    fill(64, T.posL[:], 0.0, (), ["posL"])
    pool(1, g.iota, (T.pI[:, 0:1], [[0, 1]], 0, 1), (), ["p0"])
    iota(128, T.row[:], [[1, 128]], 0, 0, (), ["row"])
    iota(256, T.posR[0:1, 0:256], [[0, 4], [32, 4], [0, 16]], 128 * r, 0, ["posR"], ["posRy"])
    iota(256, T.posR[0:1, 256:512], [[0, 16], [64, 16]], 0, 0, ["posR"], ["posRx"])
    iota(128, T.posL[32:33, :], [[0, 8], [16, 4], [0, 4]], 0, 0, ["posL"], ["posL1"])
    send(T.vnat[:, own:own + 512], 1024, "vn", ["vnat_o"], "vnat_r")
    send(T.znat[:, own:own + 512], 1024, "zn", ["znat_o"], "znat_r")
    iota(128, T.wide[:], [[1, 8], [0, 16]], 0, 0, (), ["wide"])
    act(1600, T.cb[0:1, 0:128], T.row[0:1, :], ACT.Exp, ["row"], ["cb0"], scale=0.0)
    repeat(0)
    fill(144, T.mk[:], 0.0, (), ["mk"])
    fill(600, T.lhs[:], 0.0, (), ["lhs"])
    for j in range(4):
        fill(9, T.mk[:, 12 + j:144:16], 4.0, ["mk"], [MK[j]])
        fill(9, T.mk[:, 156 + j:288:16], 1.0, ["mk"], [MK[4 + j]])
    fill(128, T.posR[32:33, 256:512], 1.0, ["posR"], ["posR1"])
    fill(128, T.posR[64:65, 256:512], 1.0, ["posR"], ["posR2"])
    fill(64, T.posL[0:1, :], 1.0, ["posL"], ["posL0"])
    fill(64, T.posL[64:65, :], 8.0, ["posL"], ["posL2"])
    vec(1, V.tensor_scalar, (T.pI[:, 1:2], T.pI[:, 0:1], 4, None, ALU.arith_shift_right), ["p0"], ["p1"])
    vec(1, V.tensor_scalar, (T.pI[:, 2:3], T.pI[:, 0:1], 1, None, ALU.arith_shift_right), ["p0"], ["p2"])
    vec(1, V.tensor_scalar, (T.pI[:, 3:4], T.pI[:, 0:1], 1, None, ALU.bitwise_and), ["p0"], ["p3"])
    vec(1, V.tensor_copy, (T.pF[:, 0:4], T.pI[:, 0:4]), ["p0", "p1", "p2", "p3"], ["pF"])
    for h in range(2):
        for kb in range(4):
            o, m = 16 + 144 * (4 * h + kb), 144 * h + 12 - 4 * kb
            vec(128, V.tensor_tensor, (T.lhs[:, o:o + 128], T.axy[:, 128 * h:128 * h + 128], T.mk[:, m:m + 128], ALU.mult),
                ["lhs", "ay" if h == 0 else "ax"] + MK, [LHS[4 * h + kb]])
    for i, x in enumerate((1.0, -1.0, 4096.0, -4096.0)):
        vec(128, V.tensor_scalar, (T.dg[:, 128 * i:128 * i + 128], T.row[:], T.pF[:, 0:1], x, ALU.is_equal, ALU.mult), ["row", "pF"], [DG[i]])
    vec(1, V.tensor_scalar, (T.pF[:, 4:5], T.pF[:, 0:1], 1.0, None, ALU.add), ["pF"], ["pF2"])
    vec(1, V.tensor_scalar, (T.pF[:, 5:6], T.pF[:, 3:4], 128.0, -128.0, ALU.mult, ALU.add), ["pF"], ["pF5"])
    vec(1, V.tensor_scalar, (T.pF[:, 6:7], T.pF[:, 3:4], 2.0, -1.0, ALU.mult, ALU.add), ["pF"], ["pF6"])
    equal(128, T.idn[:], T.row[:], 0, ["idn"])
    equal(128, T.dm[:], T.row[:], 4, ["dm"])
    equal(128, T.wide[:], T.wide[:], 0, ["wide"])
    vec(64, V.tensor_scalar, (T.j2[:], T.row[:, 0:64], T.pF[:, 2:3], T.pF[:, 6:7], ALU.is_equal, ALU.mult), ["row", "pF", "pF6"], ["j2"])
    equal(8, T.hd2[:, 0:16:2], T.row[:, 0:8], 1, ["hd2a"])
    equal(8, T.hd2[:, 1:16:2], T.row[:, 0:8], 1, ["hd2b"])
    equal(8, T.r16[:, 0:16:2], T.row[:, 0:8], 1, ["r16a"])
    equal(8, T.r16[:, 1:16:2], T.row[:, 15:128:16], 0, ["r16b"])
    fill(128, T.wide[32:33, :], 1.0, (), ["wide"])
    vec(256, V.tensor_tensor, (T.dm[:], T.dm[:], T.idn[:], ALU.subtract), ["idn"], ["dm"])
    fill(64, T.cb[0:1, 128:256], 0.0, (), ["cb1"])
    fill(512, T.us[0:64, :], 0.0, (), US)
    fill(2048 // ZS, T.msk[:], 1.0, (), ["msk"])
    fill(8, T.cb[0:1, 128:256:16], -128.0, (), ["cb1"])
    fill(256, T.us[32:33, 0:512:2], 0.5, (), US)
    fill(256 // ZS, T.msk[:, 0:4096 // ZS:16], 0.0, (), ["msk"])
    repeat(1)
    offsets(0, 0)
    offsets(0, 1)
    for c in range(16):
        if c % 2:
            vec(64, V.tensor_copy, (T.big[:, c:1024:16], T.j2[:]), ["j2"], [BIG[c]])
        else:
            act(64, T.big[:, c:1024:16], T.j2[:], ACT.Copy, ["j2"], [BIG[c]])
    R16 = ["r16a", "r16b"]
    if any(RAW):
        act(8, T.r16[:, 17:32:2], T.idn[:, 15:128:16], ACT.Copy, ["idn"], ["r16d"])
        const(8, T.r16[:, 16:32:2], T.znat[:, own:own + 8], 0.0, ["r16c"])
        act(128, T.nid[:], T.idn[:], ACT.Copy, ["idn"], ["nid"], scale=-1.0)
        R16 += ["r16c", "r16d"]

    W = [T.W0, T.W1]
    SB = [T.S0, T.S1]
    LNW = -0.25 - math.log(64.0)
    nbank = [0]

    def bank():
        nbank[0] += 1
        return nbank[0] % NW, "W%d" % (nbank[0] % NW)

    def v_layer(t):
        last = t == R - 1
        ob, vo = 256 * t, 1024 * (t % 2)
        if t == 0:
            vwin, vnm = T.vnat[:, 0:4096], ["vnat_o", "vnat_r"]
        else:
            vwin, vnm = T.vw[:, 2048 * (t - 1):2048 * (t + 1)], vslot(t - 1) + vslot(t)
        VR = ["vr%d_%d" % (t % 2, j) for j in range(4)]
        D = [["d%d_%d" % (b, kb) for kb in range(4)] for b in range(8)]
        AB = [["a%d_%d" % (b, kb) for kb in range(4)] for b in range(8)]
        raw = [b for u in RAW[t] for b in range(UNITS[u][0], sum(UNITS[u]))]
        if last:
            a0 = 2048 * t + 256 * r
            name(t, "ovo")
            act(256, T.ovb[:, 1:512:2], T.vw[:, a0:a0 + 256], ACT.Copy, vslot(t)[1:], ["ovo"])

        for u, (b, n) in enumerate(UNITS):
            for kb in range(4):
                d, src = slice(512 * b + kb, 512 * (b + n), 4), vwin.indirect(T.off[:, ob + 64 * kb + 8 * b:ob + 64 * kb + 8 * (b + n)])
                nm = [D[x][kb] for x in range(b, b + n)]
                name(t, "g%d%d" % (u, kb))
                if b in raw:
                    act(128 * n * GATH, T.dif[:, d], src, ACT.Copy, vnm + ["off%d" % t], nm)
                else:
                    vec(128 * n * GATH, V.tensor_tensor, (T.dif[:, d], src, T.vq4[:, vo + 128 * b:vo + 128 * (b + n)], ALU.subtract),
                        vnm + ["off%d" % t] + VR, nm)
                    if u in FINE:
                        name(t, "a%d%d" % (u, kb))
                        act(128 * n, T.ab[:, d], T.dif[:, d], ACT.Abs, nm, [AB[x][kb] for x in range(b, b + n)])
            for x in range(b, b + n):
                d = slice(512 * x, 512 * x + 512)
                if x in raw:
                    w, wn = bank()
                    name(t, "pre%d sub%d a%d" % (x, x, x))
                    pe(2048, [(W[w][:, kb:512:4], T.nid[:], T.vq4[:, vo + 128 * x:vo + 128 * x + 128], kb == 0, False) for kb in range(4)],
                       VR + ["nid"], [wn + "d"], [wn])
                    pe(2048, [(W[w][:], T.idn[:], T.dif[:, d], False, True)], D[x] + ["idn"], [wn + "d"], [wn])
                    act(512, T.ab[:, d], W[w][:], ACT.Abs, [wn + "d"], AB[x], [wn])
                elif u not in FINE:
                    name(t, "a%d" % x)
                    act(512, T.ab[:, d], T.dif[:, d], ACT.Abs, D[x], AB[x])

        def ratios(c):
            S, sn, cols = SB[c % 2], "S%d" % (c % 2), slice(128 * c, 128 * c + 128)
            name(t, "s%d s%d rp%d rd%d wf%d hi%d lo%d w%d h%d w%d h%d" % (2 * c, 2 * c + 1, c, c, c, c, c, 2 * c, 2 * c, 2 * c + 1, 2 * c + 1))
            for j in range(2):
                pe(1024, [(S[:, 16 * i:16 * i + 16], T.ab[:, 1024 * c + 128 * i:1024 * c + 128 * i + 128], T.hd2[:], True, True) for i in range(4 * j, 4 * j + 4)],
                   AB[2 * c + j] + ["hd2a", "hd2b"], [sn + "_%d" % j], [sn])
            act(128, T.rp[:, cols], S[:, 0:128], ACT.Relu, [sn + "_0", sn + "_1"], ["rp%d" % c], [sn], bias=0.25, scale=-1.0 / 128)
            RB, rn = [T.R0, T.R1][c % 2], "R%d" % (c % 2)
            pe(640, [(RB[:, 0:128], T.cb[0:1, 0:128], T.cb[0:1, 128:256], True, False), (RB[:, 0:128], T.rp[:, cols], T.dm[:], False, True)],
               ["rp%d" % c, "cb0", "cb1", "dm"], [rn + "d"], [rn])
            act(128, RB[:, 128:256], RB[:, 0:128], ACT.Exp, [rn + "d", "pF5"], [rn + "f"], [rn], bias=T.pF[:, 5:6])
            act(128, T.whi[:, cols], RB[:, 0:128], ACT.Exp, [rn + "d"], ["hi%d" % c], [rn])
            vec(128, V.tensor_tensor, (T.wlo[:, cols], RB[:, 128:256], T.whi[:, cols], ALU.subtract), [rn + "f", "hi%d" % c], ["lo%d" % c], [rn])
            for j in range(2):
                (w, wn), d = bank(), slice(1024 * c + 512 * j, 1024 * c + 512 * j + 512)
                pe(512, [(W[w][:, 128 * i:128 * i + 128], T.big[:, 128 * (4 * j + i):128 * (4 * j + i) + 128], T.wlo[:, cols], True, True) for i in range(4)],
                   BIG + ["lo%d" % c], [wn + "d"], [wn])
                vec(512, V.tensor_tensor_scan, (T.hs[:, d], W[w][:], T.dif[:, d], 0.0, ALU.mult, ALU.add), D[2 * c + j] + [wn + "d"], ["h%d" % (2 * c + j)], [wn])

        def finish(k, b, n):
            m, c = 32 * n, (b + n - 1) // 2
            S, sn = SB[0], "S0"
            name(t, "ew%d u%d us%d f%d tq%d fw%d fin%d %s%d" % (k, k, k, k, k, k, k, "st" if last else "send", k))
            act(m, T.ew[:, 32 * b:32 * b + m], T.rp[:, 64 * b:64 * (b + n):2], ACT.Exp, ["rp%d" % x for x in range(b // 2, c + 1)], ["ew%d" % k], bias=LNW)
            pe(256 * n, [(S[0:8, 128 + 16 * i:144 + 16 * i], T.ew[:, 32 * b + 8 * i:32 * b + 8 * i + 8], T.r16[:, 16:32] if b + i // 4 in raw else T.r16[:, 0:16],
                          True, True) for i in range(4 * n)], ["ew%d" % k] + R16, [sn + "u"], [sn])
            act(64 * n, T.us[0:8, 64 * b:64 * (b + n)], S[0:8, 128:128 + 64 * n], ACT.Copy, [sn + "u"], [US[k]], [sn])
            pe(256 * n, [(T.FB[:, 64 * b:64 * (b + n)], T.wide[0:33, :], T.us[0:33, 64 * b:64 * (b + n)], True, True)],
               [US[k], "wide"], ["fs%d" % k, "fw%d" % k], ["F"])
            tq, fw = T.tq[:, 32 * b:32 * (b + n)], T.FB[:, 64 * b + 1:64 * (b + n):2]
            vec(m, V.tensor_tensor, (tq, T.FB[:, 64 * b:64 * (b + n):2], T.vq4[:, vo + 128 * b:vo + 128 * (b + n):4], ALU.mult),
                ["fs%d" % k] + VR, ["tq%d" % k], ["F"])
            vec(m, V.tensor_tensor, (fw, fw, T.hs[:, 512 * b + 15:512 * (b + n):16], ALU.mult), ["h%d" % x for x in range(b, b + n)], ["fw%d" % k], ["F"])
            if last:
                vec(m, V.tensor_tensor, (T.ovb[:, 64 * b:64 * (b + n):2], fw, tq, ALU.add), ["tq%d" % k, "fw%d" % k], ["ove%d" % k], ["F"])
                dma("sp", "st%d" % k, T.yv[:, 64 * b:64 * (b + n)], T.ovb[:, 64 * b:64 * (b + n)], ["ove%d" % k, "ovo"], ())
            else:
                o, nm = T.vw[:, 2048 * (t + 1) + 256 * r + 32 * b:2048 * (t + 1) + 256 * r + 32 * (b + n)], "vs%d_o%d" % (t + 1, k)
                vec(m, V.tensor_tensor, (o, fw, tq, ALU.add), ["tq%d" % k, "fw%d" % k], [nm], ["F"])
                send(o, 4 * m, "av%d" % t, [nm], "vs%d_r" % (t + 1))

        for k, (b, n) in enumerate(GROUPS):
            for c in range(b // 2, (b + n) // 2):
                ratios(c)
            finish(k, b, n)

    def z_layer(t):
        if t == 0:
            zwin, znm = T.znat[:, 0:4096], ["znat_o", "znat_r"]
        else:
            zwin, znm = T.zw[:, 2048 * (t - 1):2048 * (t + 1)], zslot(t - 1) + zslot(t)
        n, s = 4096 // ZG, 4096 // ZS
        for c in range(ZG):
            for kb in range(4):
                o = 256 * t + 64 * kb + n // 64 * c
                out, src = T.zg[:, n * c + kb:n * c + n:4], zwin.indirect(T.off[:, o:o + n // 64])
                name(t, "zg%d" % (4 * c + kb))
                if 4 * c + kb in ZV[t]:
                    vec(n // 4 * GATH, V.tensor_copy, (out, src), znm + ["off%d" % t], ["zg%d_%d" % (c, kb)])
                else:
                    act(n // 4 * GATH, out, src, ACT.Copy, znm + ["off%d" % t], ["zg%d_%d" % (c, kb)])
        for i in range(ZS):
            name(t, "zm%d" % i)
            vec(s // 2, V.tensor_tensor_scan, (T.zs[:, s * i:s * i + s], T.msk[:], T.zg[:, s * i:s * i + s], 0.0, ALU.mult, ALU.max),
                ["msk"] + ["zg%d_%d" % (i * ZG // ZS, k) for k in range(4)], ["zm%d" % i])
        name(t, "mix bI cI")
        pe(256, [(T.R1[:, 256:512], T.bms[:], T.zs[:, 15:4096:16], True, True)], ["bm"] + ["zm%d" % i for i in range(ZS)], ["mix"], ["R1"])
        vec(256, V.tensor_copy, (T.bI[:], T.R1[:, 256:512]), ["mix"], ["bI"], ["R1"])
        vec(256, V.tensor_scalar, (T.cI[:], T.bI[:], 2, 15, ALU.arith_shift_right, ALU.bitwise_and), ["bI"], ["cI"])
        if t == R - 1:
            a0 = 2048 * t + 256 * r
            name(t, "ozo zo stz")
            act(256, T.ozb[:, 1:512:2], T.zw[:, a0:a0 + 256], ACT.Copy, ["zs%d_o" % t], ["ozo"])
            vec(256, V.tensor_copy, (T.ozb[:, 0:512:2], T.cI[:]), ["cI"], ["oze"])
            dma("sp", "stz", T.yz[:], T.ozb[:], ["oze", "ozo"], ())
        else:
            a0 = 2048 * (t + 1) + 256 * r
            name(t, "zo sendz")
            vec(256, V.tensor_copy, (T.zw[:, a0:a0 + 256], T.cI[:]), ["cI"], ["zs%d_o" % (t + 1)])
            send(T.zw[:, a0:a0 + 256], 512, "az%d" % t, ["zs%d_o" % (t + 1)], "zs%d_r" % (t + 1))

    for t in range(R):
        v_layer(t)
        if t == 0:
            odd(T.vw, T.vnat, "v")
        if t < R - 1:
            offsets(t + 1, 0)
            offsets(t + 1, 1)
        if 1 <= t < R - 1:
            repeat(t + 1)
        z_layer(t)
        if t == 0:
            odd(T.zw, T.znat, "z")

    if not ORDER:
        ORDER.extend(schedule(steps, keys(steps, group)))
    cnt = {"pe": 0, "dve": 0, "act": 0, "pool": 0, "sent": 0}
    clock = {q: {} for q in Q}
    writer, readers, touch = {}, {}, {}
    for kind, *rest in calls:
        if kind == "wire":
            v = neng * (NR - 1) + (writer[rest[1]][0][1] if rest[1] in writer else 0)
            writer[rest[1]] = [(rest[0], v, {rest[0]: v})]

    def sync(q, reads, writes, banks):
        need = []
        for x in reads:
            need += writer[x]
        for x in writes:
            need += writer.get(x, []) + readers.get(x, [])
        for b in banks:
            need += [tok for e, tok in touch.get(b, {}).items() if e != q]
        best = {}
        for tok in need:
            if q == "pe" and tok[0] == "pe":
                continue
            if tok[0] not in best or best[tok[0]][1] < tok[1]:
                best[tok[0]] = tok
        ck = clock[q]
        for tok in sorted(best.values(), key=lambda k: -len(k[2])):
            if ck.get(tok[0], 0) >= tok[1]:
                continue
            Q[q].wait_ge(T.sem[tok[0]], tok[1])
            for s, v in tok[2].items():
                if ck.get(s, 0) < v:
                    ck[s] = v

    def note(q, sem, v, reads, writes, banks):
        tok = (sem, v, dict(clock[q], **{sem: v}))
        for x in reads:
            readers.setdefault(x, []).append(tok)
        for x in writes:
            writer[x] = [tok]
            readers[x] = []
        for b in banks:
            touch.setdefault(b, {})[q] = tok

    for i in ORDER:
        q, _, _, reads, writes, banks = steps[i]
        kind, *rest = calls[i]
        if kind == "op":
            if q == "pool":
                writes = writes + ["poolq"]
            sync(q, reads, writes, banks)
            rest[0](*rest[1], **rest[2]).then_inc(T.sem[q], 1)
            cnt[q] += 1
            note(q, q, cnt[q], reads, writes, banks)
        elif kind == "dma":
            sync(q, reads, writes, ())
            Q[q].dma_start(rest[1], rest[2]).then_inc(T.sem[rest[0]], 16)
            note(q, rest[0], 16, reads, writes, ())
        elif kind == "send":
            sync(q, reads, (), ())
            g.remote_dma_fused([RemoteDMATransfer(dst_ids=ids, dma_engine_mask=emask, remote_sem=T.sem[rest[1]], src=rest[0],
                                                  dsts=[rest[0]] * len(ids))], local_sem=T.sem.sent)
            cnt["sent"] += neng

    for s in ("pe", "dve", "act", "pool", "sent"):
        g.wait_ge(T.sem[s], cnt[s])
    for s in ["stz"] + ["st%d" % c for c in range(NG)]:
        g.wait_ge(T.sem[s], 16)
